import numpy as np
import ml_dtypes


def mxq(x, axis, fmt="e4m3"):
    dtype, down = {"e4m3": (ml_dtypes.float8_e4m3fn, 7), "e5m2": (ml_dtypes.float8_e5m2, 14)}[fmt]
    v = np.moveaxis(np.asarray(x, np.float32).astype(ml_dtypes.bfloat16).astype(np.float64), axis, -1)
    blocks = v.reshape(v.shape[:-1] + (-1, 32))
    amax = np.abs(blocks).max(-1, keepdims=True)
    byte = np.maximum(np.where(amax > 0, np.frexp(amax)[1] - 1 + 127, 0) - down, 1)
    scale = np.exp2(byte - 127.0)
    codes = (blocks / scale).astype(np.float32).astype(dtype).astype(np.float64)
    return np.moveaxis((codes * scale).reshape(v.shape), -1, axis)


WIDE = False


def mx_kscale(k):
    if not WIDE:
        return np.ones(k)
    levels = np.array([10, -10, 5, -5, 0])
    if k % 512:
        return np.exp2(np.random.permutation(np.resize(levels, k // 32))).repeat(32)
    a = np.empty((k // 512, 16))
    for p in range(k // 512):
        a[p, :8] = np.random.permutation(np.resize(levels, 8))
        for g in range(8):
            far = levels[np.abs(levels - a[p, g]) >= 10]
            a[p, g + 8] = far[np.random.randint(len(far))]
    return np.exp2(a.ravel()).repeat(32)


BF16 = ml_dtypes.bfloat16


def bf(x):
    return np.asarray(x, np.float32).astype(BF16)


def f64(x):
    return np.asarray(x).astype(np.float64)


E2M1 = np.array([0.0, 0.5, 1.0, 1.5, 2.0, 3.0, 4.0, 6.0, -0.0, -0.5, -1.0, -1.5, -2.0, -3.0, -4.0, -6.0])


def pack_weight(w, fmt):
    k, n = w.shape
    w = f64(bf(w)).reshape(k // 32, 32, n)
    amax = np.abs(w).max(1)
    if fmt == "e4m3":
        byte = np.frexp(amax)[1] - 1 + 127 - 7
    else:
        mant, ex = np.frexp(amax / 6.0)
        byte = np.where(mant > 0.5, ex, ex - 1) + 127
    byte = np.clip(np.where(amax > 0, byte, 1), 1, 254)
    scaled = (w * np.exp2(127.0 - byte)[:, None, :]).reshape(k, n).astype(np.float32)
    by_word = np.ascontiguousarray(scaled.reshape(k // 512, 128, 4, n).transpose(0, 1, 3, 2))
    if fmt == "e4m3":
        words = by_word.astype(ml_dtypes.float8_e4m3fn).view(np.uint8)
    else:
        c = by_word.astype(ml_dtypes.float4_e2m1fn).view(np.uint8) & 0xF
        words = c[..., 0::2] | (c[..., 1::2] << 4)
    return np.ascontiguousarray(words), np.ascontiguousarray(byte.astype(np.uint8).reshape(k // 512, 16, n))


def unpack_weight(words, scales, fmt):
    g, p, n, _ = words.shape
    if fmt == "e4m3":
        vals = np.ascontiguousarray(words).view(ml_dtypes.float8_e4m3fn).astype(np.float64)
    else:
        nib = np.empty((g, p, n, 4), np.uint8)
        nib[..., 0::2] = words & 0xF
        nib[..., 1::2] = words >> 4
        vals = E2M1[nib]
    vals = vals * np.repeat(np.exp2(scales.astype(np.float64) - 127.0), 8, axis=1)[..., None]
    return vals.transpose(0, 1, 3, 2).reshape(g * 512, n)
def pack4(w):
    words, scales = pack_weight(w, "e2m1")
    return words.reshape(words.shape[0], 128, -1), scales


def unpack4(words, scales):
    return unpack_weight(words.reshape(words.shape[0], 128, -1, 2), scales, "e2m1")


N, D, F, L, Q = 1024, 1024, 1024, 512, 512


def draw0():
    a, b, u = mx_kscale(D), mx_kscale(L), mx_kscale(N)
    lam = np.random.uniform(0.5, 1.5, F)
    x = bf(np.random.standard_normal((N, D)) * a)
    w_words, w_scales = pack4(np.random.standard_normal((D, F)) * lam / np.sqrt(D) / a[:, None])
    s = bf((1.0 + 0.3 * np.random.standard_normal(N)) * u)
    t = bf(np.random.standard_normal((N, Q)) / u[:, None])
    g = bf(np.random.standard_normal((N, L)) * b / u[:, None])
    beta_words, beta_scales = pack4(np.random.standard_normal((L, Q)) / np.sqrt(L) / b[:, None])
    tau = bf(np.random.uniform(0.5, 1.5, Q))
    return {
        "x": x,
        "w_words": w_words,
        "w_scales": w_scales,
        "s": s,
        "t": t,
        "g": g,
        "beta_words": beta_words,
        "beta_scales": beta_scales,
        "tau": tau,
    }


def candidate_nodes(x, w_words, w_scales):
    return np.tanh(mxq(f64(x), 1, "e4m3") @ unpack4(w_words, w_scales))


def network_residual(t, g, beta_words, beta_scales):
    return f64(t) - (mxq(f64(g), 1, "e4m3") @ unpack4(beta_words, beta_scales))


def core(x, w_words, w_scales, s, t, g, beta_words, beta_scales, tau):
    h = candidate_nodes(x, w_words, w_scales)
    e = network_residual(t, g, beta_words, beta_scales)
    hs = f64(s)[:, None] * h
    c = mxq(hs, 0, "e4m3").T @ mxq(e, 0, "e4m3")
    hh = np.sum(np.square(h), axis=0)
    return np.square(c) / hh[:, None] - f64(tau)[None, :]


def e4m3fn_bytes(y):
    return np.clip(np.asarray(y, np.float64), -448.0, 448.0).astype(np.float32).astype(ml_dtypes.float8_e4m3fn).view(np.uint8)


def e4m3fn_values(b):
    return np.asarray(b, np.uint8).view(ml_dtypes.float8_e4m3fn).astype(np.float64)


def setup_inputs():
    d = draw0()
    x0 = np.asarray(d['x']).astype(np.float64)
    s = (np.max(np.abs(x0), axis=(0,), keepdims=True) / 448.0).astype(np.float32)
    out = {}
    for k, v in d.items():
        if k == 'x':
            out['x_bytes'] = e4m3fn_bytes(x0 / s.astype(np.float64))
            out['x_scale'] = s
        else:
            out[k] = v
    return out


def reference(x_bytes, x_scale, w_words, w_scales, s, t, g, beta_words, beta_scales, tau):
    return core(e4m3fn_values(x_bytes) * x_scale.astype(np.float64), w_words, w_scales, s, t, g, beta_words, beta_scales, tau)

@@ -1,0 +1,323 @@
+from contextlib import ExitStack
+
+import concourse.mybir as mybir
+from concourse.masks import make_identity
+
+F32 = mybir.dt.float32
+BF16 = mybir.dt.bfloat16
+I32 = mybir.dt.int32
+U32 = mybir.dt.uint32
+U8 = mybir.dt.uint8
+FP8 = mybir.dt.float8_e4m3fn
+FP8X4 = mybir.dt.float8_e4m3fn_x4
+FP4X4 = mybir.dt.float4_e2m1fn_x4
+ACT = mybir.ActivationFunctionType
+ALU = mybir.AluOpType
+
+N, D, F, L, Q = 1024, 1024, 1024, 512, 512
+FLOPS = 2 * N * D * F + 2 * N * L * Q + 2 * N * F * Q
+P = 128
+X_LOADS = [1, 1, 2, 2, 2]
+TR, MM, EC = 4, 2, 2
+ORDER = [
+    ("castS", 0, 1), ("castS", 3, 1), ("castV", 0, 0), ("castS", 2, 1), ("castV", 1, 0), ("castV", 1, 1),
+    ("xT", 0, 0), ("xT", 1, 0), ("xT", 1, 1), ("castS", 3, 0), ("xE", 0, 0), ("xT", 0, 1), ("xE", 1, 0),
+    ("xE", 1, 1), ("castS", 2, 0), ("xE", 0, 1), ("xT", 3, 0), ("xT", 3, 1), ("xT", 2, 0), ("xQ", 1), ("xQ", 0),
+    ("castV", 5, 0), ("mm", 1, 0), ("castS", 5, 1), ("xE", 3, 1), ("xT", 5, 0), ("xT", 2, 1), ("xE", 3, 0),
+    ("castS", 6, 0), ("mm", 0, 0), ("castS", 4, 0), ("xE", 2, 1), ("gT", 0), ("xE", 2, 0), ("xT", 6, 0),
+    ("gT", 1), ("castS", 7, 0), ("castS", 4, 1), ("castS", 6, 1), ("xQ", 3), ("xE", 5, 0), ("tanh", 1, 0),
+    ("xT", 5, 1), ("tanh", 0, 0), ("gE", 1), ("xT", 6, 1), ("xE", 6, 0), ("mm", 3, 0), ("xQ", 2), ("mm", 2, 0),
+    ("xE", 5, 1), ("xT", 4, 0), ("castS", 7, 1), ("gE", 0), ("tanh", 3, 0), ("xT", 7, 0), ("xE", 6, 1),
+    ("gQ", 1), ("xT", 4, 1), ("xE", 4, 0), ("xQ", 5), ("xT", 7, 1), ("gT", 2), ("tanh", 2, 0), ("gE", 2),
+    ("xE", 4, 1), ("xE", 7, 1), ("xE", 7, 0), ("mm", 5, 0), ("xQ", 4), ("tanh", 5, 0), ("gT", 3),
+    ("hT", 0, 0, 3), ("gE", 3), ("hT", 0, 0, 1), ("hT", 0, 0, 2), ("mm", 1, 1), ("mm", 4, 0), ("gQ", 0),
+    ("beta", 0, 1), ("gQ", 2), ("gQ", 3), ("xQ", 6), ("beta", 1, 1), ("xQ", 7), ("mm", 6, 0), ("hs", 0, 0, 0),
+    ("es", 0, 1), ("mm", 0, 1), ("hs", 0, 0, 1), ("beta", 0, 0), ("tanh", 1, 1), ("mm", 7, 0), ("mm", 3, 1),
+    ("hT", 0, 0, 0), ("tanh", 4, 0), ("sq", 0, 0, 3), ("es", 0, 0), ("tanh", 6, 0), ("tanh", 0, 1),
+    ("mm", 2, 1), ("mm", 4, 1), ("tanh", 7, 0), ("hQ", 0, 0, 1), ("hT", 0, 1, 1), ("tanh", 3, 1),
+    ("beta", 0, 2), ("beta", 0, 3), ("mm", 7, 1), ("hQ", 0, 0, 0), ("sq", 0, 0, 1), ("es", 1, 1),
+    ("tanh", 2, 1), ("sq", 0, 0, 0), ("hs", 0, 1, 0), ("sq", 0, 0, 2), ("tanh", 4, 1), ("sq", 0, 1, 1),
+    ("hs", 0, 1, 1), ("hT", 1, 0, 3), ("hT", 1, 0, 2), ("hT", 0, 1, 2), ("es", 0, 2), ("tanh", 7, 1),
+    ("hT", 0, 1, 3), ("sq", 1, 0, 2), ("mm", 6, 1), ("es", 0, 3), ("hs", 1, 0, 0), ("sq", 1, 0, 3),
+    ("beta", 1, 2), ("beta", 1, 3), ("eQ", 0), ("mm", 5, 1), ("beta", 1, 0), ("es", 1, 2), ("es", 1, 3),
+    ("tanh", 6, 1), ("hT", 1, 0, 1), ("sq", 0, 1, 3), ("sq", 0, 1, 2), ("hQ", 0, 1, 0), ("hT", 0, 1, 0),
+    ("tanh", 5, 1), ("es", 1, 0), ("hQ", 0, 1, 1), ("sq", 1, 0, 1), ("hT", 1, 0, 0), ("eQ", 1), ("c0", 0, 2),
+    ("c0", 0, 3), ("hT", 1, 1, 1), ("c1", 0, 2), ("sq", 0, 1, 0), ("hs", 1, 0, 1), ("c1", 0, 3),
+    ("hT", 1, 1, 0), ("rec", 0), ("hs", 1, 1, 0), ("hT", 1, 1, 2), ("sq", 1, 0, 0), ("csq", 0, 2),
+    ("hT", 1, 1, 3), ("c0", 0, 1), ("c0", 0, 0), ("csq", 0, 3), ("sq", 1, 1, 1), ("hs", 1, 1, 1),
+    ("hQ", 1, 0, 0), ("c1", 0, 1), ("sq", 1, 1, 2), ("csq", 0, 1), ("hQ", 1, 1, 0), ("hQ", 1, 0, 1),
+    ("c1", 0, 0), ("out", 0, 3), ("csq", 0, 0), ("c0", 1, 1), ("c1", 1, 1), ("sq", 1, 1, 3), ("c0", 1, 2),
+    ("sq", 1, 1, 0), ("csq", 1, 1), ("hQ", 1, 1, 1), ("out", 0, 1), ("c1", 1, 2), ("c0", 1, 0), ("out", 0, 0),
+    ("rec", 1), ("c1", 1, 0), ("out", 0, 2), ("c0", 1, 3), ("csq", 1, 2), ("c1", 1, 3), ("out", 1, 2),
+    ("csq", 1, 0), ("out", 1, 1), ("out", 1, 0), ("csq", 1, 3), ("out", 1, 3),
+]
+
+
+def tile_stochasticconfigurationcandidatescores_w4_kernel(
+    tc, x_bytes, x_scale, w_words, w_scales, s, t, g, beta_words, beta_scales, tau, out
+):
+    nc = tc.nc
+    with ExitStack() as ctx:
+        keep = ctx.enter_context(tc.tile_pool(name="keep", bufs=1))
+        psum = ctx.enter_context(tc.psum_pool(name="psum", bufs=1))
+
+        def kt(name, shape, dt):
+            return keep.tile(shape, dt, name=name, align_bytes=64)
+
+        ident = kt("ident", [P, P], F32)
+        warm = kt("warm", [P, 2], F32)
+        xs = [kt("xs%d" % h, [P, n, D], U8) for h, n in enumerate(X_LOADS)]
+        xrow = {}
+        for h, n in enumerate(X_LOADS):
+            for i in range(n):
+                xrow[sum(X_LOADS[:h]) + i] = (h, i)
+        xb = [kt("xb%d" % r, [P, D], BF16) for r in range(8)]
+        xsc = kt("xsc", [P, 2, 4], F32)
+        xg = [kt("xg%d" % r, [P, 2, P, 4], BF16) for r in range(8)]
+        xcod = [kt("xcod%d" % r, [P, 2, P], U32) for r in range(8)]
+        xcsc = [kt("xcsc%d" % r, [P, 2, P], U8) for r in range(8)]
+        wwd = [kt("wwd%d" % h, [P, 2, 1024], U8) for h in range(2)]
+        wsc = kt("wsc", [P, 2, F], U8)
+        bwd = kt("bwd", [P, 2 * Q], U8)
+        bsc = kt("bsc", [P, Q], U8)
+        gs = [kt("gs%d" % h, [P, 4, L], BF16) for h in range(2)]
+        gg = [kt("gg%d" % j, [P, 2, P, 4], BF16) for j in range(4)]
+        gcod = [kt("gcod%d" % j, [P, 2, P], U32) for j in range(4)]
+        gcsc = [kt("gcsc%d" % j, [P, 2, P], U8) for j in range(4)]
+        ts = [kt("ts%d" % h, [P, 4, Q], BF16) for h in range(2)]
+        s4 = kt("s4", [P, 2, 4], BF16)
+        taub = kt("taub", [P, Q], BF16)
+        eb = [kt("eb%d" % h, [P, Q, 4], BF16) for h in range(2)]
+        ecod = [kt("ecod%d" % h, [P, Q], U32) for h in range(2)]
+        ecsc = [kt("ecsc%d" % h, [P, Q], U8) for h in range(2)]
+        hh = {}
+        hsb = {}
+        hcod = {}
+        hcsc = {}
+        for f in range(2):
+            for gi in range(2):
+                hh[f, gi] = kt("h%d%d" % (f, gi), [P, 4, 512], F32)
+                hsb[f, gi] = kt("hs%d%d" % (f, gi), [P, 512, 4], BF16)
+                hcod[f, gi] = kt("hcod%d%d" % (f, gi), [P, 512], U32)
+                hcsc[f, gi] = kt("hcsc%d%d" % (f, gi), [P, 512], U8)
+        part = [kt("part%d" % f, [P, 4, 2], F32) for f in range(2)]
+        hsum = [kt("hsum%d" % f, [P, 4], F32) for f in range(2)]
+        rinv = [kt("rinv%d" % f, [P, 4], F32) for f in range(2)]
+        junk = kt("junk", [P, 512], BF16)
+        csqs = [kt("csq%d" % i, [P, Q], F32) for i in range(8)]
+        outs = [kt("out%d" % i, [P, Q], F32) for i in range(8)]
+
+        banks = {}
+
+        def bank(tag, key, bufs):
+            banks[key] = psum.tile([P, 512], F32, name="ps_" + tag, tag=tag, bufs=bufs)
+            return banks[key]
+
+        def cast_s(r, gk):
+            h, i = xrow[r]
+            sl = slice(gk * 512, (gk + 1) * 512)
+            nc.scalar.copy(xb[r][:, sl], xs[h][:, i, sl].bitcast(FP8))
+
+        def cast_v(r, gk):
+            h, i = xrow[r]
+            sl = slice(gk * 512, (gk + 1) * 512)
+            nc.vector.tensor_copy(out=xb[r][:, sl], in_=xs[h][:, i, sl].bitcast(FP8))
+
+        def x_t(r, gk):
+            if gk == 0:
+                bank("tr", ("x", r), TR)
+            b = banks["x", r]
+            words = xb[r][:].bitcast(F32)
+            for u in range(2):
+                i = 2 * gk + u
+                nc.tensor.transpose(b[:, i * P : (i + 1) * P], words[:, 256 * gk + u : 256 * (gk + 1) : 2], ident[:])
+
+        def x_e(r, gk):
+            b = banks["x", r]
+            src = b[:, gk * 256 : (gk + 1) * 256].bitcast(BF16).rearrange("p (u r e) -> p r u e", u=2, e=2)
+            sc = xsc[:, gk, :].rearrange("p (u e) -> p u e", u=2).unsqueeze(1).to_broadcast([P, P, 2, 2])
+            dst = xg[r][:, gk].rearrange("p r (u e) -> p r u e", u=2)
+            nc.vector.tensor_tensor(out=dst, in0=src, in1=sc, op=ALU.mult)
+
+        def x_q(r):
+            nc.vector.quantize_mx(
+                out=xcod[r][:].rearrange("p g r -> p (g r)").bitcast(FP8X4),
+                scales=xcsc[r][:].rearrange("p g r -> p (g r)"),
+                in_=xg[r][:].rearrange("p g r k -> p (g r k)"),
+            )
+
+        def mm(r, f):
+            b = bank("mm", ("m", r, f), MM)
+            for gk in range(2):
+                nc.tensor.matmul_mx(
+                    out=b[:],
+                    lhsT=xcod[r][:, gk, :].bitcast(FP8X4),
+                    lhsT_scale=xcsc[r][:, gk, :],
+                    rhs=wwd[f][:, gk, :].bitcast(FP4X4),
+                    rhs_scale=wsc[:, gk, f * 512 : (f + 1) * 512],
+                    start=(gk == 0),
+                    stop=(gk == 1),
+                )
+
+        def tanh(r, f):
+            nc.scalar.activation(out=hh[f, r // 4][:, r % 4, :], in_=banks["m", r, f][:], func=ACT.Tanh)
+
+        def g_t(j):
+            b = bank("tr", ("g", j), TR)
+            for i in range(2):
+                words = gs[j // 2][:, 2 * (j % 2) + i, :].bitcast(F32)
+                for u in range(2):
+                    k = 2 * i + u
+                    nc.tensor.transpose(b[:, k * P : (k + 1) * P], words[:, u:256:2], ident[:])
+
+        def g_e(j):
+            nc.scalar.copy(
+                gg[j][:].bitcast(F32),
+                banks["g", j][:].rearrange("p (i u r) -> p i r u", i=2, u=2),
+            )
+
+        def g_q(j):
+            nc.vector.quantize_mx(
+                out=gcod[j][:].rearrange("p i r -> p (i r)").bitcast(FP8X4),
+                scales=gcsc[j][:].rearrange("p i r -> p (i r)"),
+                in_=gg[j][:].rearrange("p i r k -> p (i r k)"),
+            )
+
+        def beta(gi, qb):
+            b = bank("ec", ("b", gi, qb), EC)
+            for tt in range(4):
+                j, i = 2 * gi + tt // 2, tt % 2
+                nc.tensor.matmul_mx(
+                    out=b[:, tt * P : (tt + 1) * P],
+                    lhsT=gcod[j][:, i, :].bitcast(FP8X4),
+                    lhsT_scale=gcsc[j][:, i, :],
+                    rhs=bwd[:, qb * 256 : (qb + 1) * 256].bitcast(FP4X4),
+                    rhs_scale=bsc[:, qb * P : (qb + 1) * P],
+                    start=True,
+                    stop=True,
+                )
+
+        def e_s(gi, qb):
+            nc.vector.tensor_tensor(
+                out=eb[gi][:, qb * P : (qb + 1) * P, :],
+                in0=ts[gi][:, :, qb * P : (qb + 1) * P].rearrange("p t q -> p q t"),
+                in1=banks["b", gi, qb][:].rearrange("p (t q) -> p q t", t=4),
+                op=ALU.subtract,
+            )
+
+        def e_q(gi):
+            nc.vector.quantize_mx(
+                out=ecod[gi][:].bitcast(FP8X4), scales=ecsc[gi][:], in_=eb[gi][:].rearrange("p q t -> p (q t)")
+            )
+
+        def h_t(f, gi, fb):
+            b = bank("tr", ("h", f, gi, fb), TR)
+            for tt in range(4):
+                nc.tensor.transpose(b[:, tt * P : (tt + 1) * P], hh[f, gi][:, tt, fb * P : (fb + 1) * P], ident[:])
+
+        def sq(f, gi, fb):
+            nc.scalar.activation(
+                out=junk[:], in_=banks["h", f, gi, fb][:], func=ACT.Square, accum_out=part[f][:, fb, gi : gi + 1]
+            )
+
+        def hs(f, gi, half):
+            sl = slice(half * 256, (half + 1) * 256)
+            nc.vector.tensor_tensor(
+                out=hsb[f, gi][:, sl, :].rearrange("p (c i) t -> p c t i", i=4),
+                in0=hh[f, gi][:, :, sl].rearrange("p t (c i) -> p c t i", i=4),
+                in1=s4[:, gi, :].unsqueeze(1).unsqueeze(3).to_broadcast([P, 64, 4, 4]),
+                op=ALU.mult,
+            )
+
+        def h_q(f, gi, half):
+            sl = slice(half * 256, (half + 1) * 256)
+            nc.vector.quantize_mx(
+                out=hcod[f, gi][:, sl].bitcast(FP8X4),
+                scales=hcsc[f, gi][:, sl],
+                in_=hsb[f, gi][:, sl, :].rearrange("p f t -> p (f t)"),
+            )
+
+        def rec(f):
+            nc.vector.tensor_tensor(out=hsum[f][:], in0=part[f][:, :, 0], in1=part[f][:, :, 1], op=ALU.add)
+            nc.vector.reciprocal(out=rinv[f][:], in_=hsum[f][:])
+
+        def c_mm(gi, f, fb):
+            if gi == 0:
+                bank("ec", ("c", f, fb), EC)
+            nc.tensor.matmul_mx(
+                out=banks["c", f, fb][:],
+                lhsT=hcod[f, gi][:, fb * P : (fb + 1) * P].bitcast(FP8X4),
+                lhsT_scale=hcsc[f, gi][:, fb * P : (fb + 1) * P],
+                rhs=ecod[gi][:].bitcast(FP8X4),
+                rhs_scale=ecsc[gi][:],
+                start=(gi == 0),
+                stop=(gi == 1),
+            )
+
+        def c0(f, fb):
+            c_mm(0, f, fb)
+
+        def c1(f, fb):
+            c_mm(1, f, fb)
+
+        def c_sq(f, fb):
+            nc.scalar.activation(out=csqs[4 * f + fb][:], in_=banks["c", f, fb][:], func=ACT.Square)
+
+        def o(f, fb):
+            k = 4 * f + fb
+            nc.vector.scalar_tensor_tensor(
+                out=outs[k][:], in0=csqs[k][:], scalar=rinv[f][:, fb : fb + 1], in1=taub[:], op0=ALU.mult, op1=ALU.subtract
+            )
+            nc.sync.dma_start(out=out[k * P : (k + 1) * P, :], in_=outs[k][:])
+
+        STEP = {
+            "castS": cast_s, "castV": cast_v, "xT": x_t, "xE": x_e, "xQ": x_q, "mm": mm, "tanh": tanh,
+            "gT": g_t, "gE": g_e, "gQ": g_q, "beta": beta, "es": e_s, "eQ": e_q, "hT": h_t, "sq": sq,
+            "hs": hs, "hQ": h_q, "rec": rec, "c0": c0, "c1": c1, "csq": c_sq, "out": o,
+        }
+
+        make_identity(nc, ident[:])
+        nc.vector.memset(warm[:], 0.0)
+        nc.scalar.activation(out=warm[:, 1:2], in_=warm[:, 0:1], func=ACT.Tanh)
+        nc.vector.memset(wsc[:].rearrange("p g n -> p (g n)").bitcast(I32), 0)
+        nc.vector.memset(bsc[:].bitcast(I32), 0)
+
+        xv = x_bytes.rearrange("(g p t) k -> g p t k", p=P, t=4)
+        ld = nc.sync.dma_start
+
+        def ldx(h):
+            r0 = sum(X_LOADS[:h])
+            ld(out=xs[h][:], in_=xv[r0 // 4][:, r0 % 4 : r0 % 4 + X_LOADS[h], :])
+
+        ldx(0)
+        ldx(1)
+        ld(out=xsc[:], in_=x_scale.rearrange("o (g p t) -> p (o g) t", p=P, t=4))
+        ldx(2)
+        for qd in range(4):
+            ld(
+                out=wsc[32 * qd : 32 * qd + 4, :, :].bitcast(I32),
+                in_=w_scales[:, 4 * qd : 4 * qd + 4, :].rearrange("g r n -> r g n").bitcast(I32),
+            )
+        wv = w_words.rearrange("g p n -> p g n")
+        ld(out=wwd[0][:].bitcast(I32), in_=wv[:, :, 0:1024].bitcast(I32))
+        for h in range(3, len(X_LOADS)):
+            ldx(h)
+        ld(out=s4[:], in_=s.rearrange("(g p t) -> p g t", p=P, t=4))
+        ld(out=wwd[1][:].bitcast(I32), in_=wv[:, :, 1024:2048].bitcast(I32))
+        for qd in range(4):
+            ld(
+                out=bsc[32 * qd : 32 * qd + 4, :].bitcast(I32),
+                in_=beta_scales[0][4 * qd : 4 * qd + 4, :].bitcast(I32),
+            )
+        ld(out=bwd[:].bitcast(I32), in_=beta_words[0].bitcast(I32))
+        gv = g.rearrange("(g p t) k -> g p t k", p=P, t=4)
+        tv = t.rearrange("(g p t) k -> g p t k", p=P, t=4)
+        ld(out=gs[0][:], in_=gv[0])
+        ld(out=ts[0][:], in_=tv[0])
+        ld(out=gs[1][:], in_=gv[1])
+        ld(out=ts[1][:], in_=tv[1])
+        ld(out=taub[:], in_=tau.partition_broadcast(P))
+
+        with tc.manual_schedule(engines={mybir.EngineType.PE, mybir.EngineType.Activation, mybir.EngineType.DVE}):
+            for st in ORDER:
+                STEP[st[0]](*st[1:])

@@ -17,39 +17,40 @@ ALU = mybir.AluOpType
 N, D, F, L, Q = 1024, 1024, 1024, 512, 512
 FLOPS = 2 * N * D * F + 2 * N * L * Q + 2 * N * F * Q
 P = 128
-X_LOADS = [1, 1, 2, 2, 2]
+X_LOADS = [1, 1, 2, 4]
 TR, MM, EC = 4, 2, 2
 ORDER = [
-    ("castS", 0, 1), ("castS", 3, 1), ("castV", 0, 0), ("castS", 2, 1), ("castV", 1, 0), ("castV", 1, 1),
-    ("xT", 0, 0), ("xT", 1, 0), ("xT", 1, 1), ("castS", 3, 0), ("xE", 0, 0), ("xT", 0, 1), ("xE", 1, 0),
-    ("xE", 1, 1), ("castS", 2, 0), ("xE", 0, 1), ("xT", 3, 0), ("xT", 3, 1), ("xT", 2, 0), ("xQ", 1), ("xQ", 0),
-    ("castV", 5, 0), ("mm", 1, 0), ("castS", 5, 1), ("xE", 3, 1), ("xT", 5, 0), ("xT", 2, 1), ("xE", 3, 0),
-    ("castS", 6, 0), ("mm", 0, 0), ("castS", 4, 0), ("xE", 2, 1), ("gT", 0), ("xE", 2, 0), ("xT", 6, 0),
-    ("gT", 1), ("castS", 7, 0), ("castS", 4, 1), ("castS", 6, 1), ("xQ", 3), ("xE", 5, 0), ("tanh", 1, 0),
-    ("xT", 5, 1), ("tanh", 0, 0), ("gE", 1), ("xT", 6, 1), ("xE", 6, 0), ("mm", 3, 0), ("xQ", 2), ("mm", 2, 0),
-    ("xE", 5, 1), ("xT", 4, 0), ("castS", 7, 1), ("gE", 0), ("tanh", 3, 0), ("xT", 7, 0), ("xE", 6, 1),
-    ("gQ", 1), ("xT", 4, 1), ("xE", 4, 0), ("xQ", 5), ("xT", 7, 1), ("gT", 2), ("tanh", 2, 0), ("gE", 2),
-    ("xE", 4, 1), ("xE", 7, 1), ("xE", 7, 0), ("mm", 5, 0), ("xQ", 4), ("tanh", 5, 0), ("gT", 3),
-    ("hT", 0, 0, 3), ("gE", 3), ("hT", 0, 0, 1), ("hT", 0, 0, 2), ("mm", 1, 1), ("mm", 4, 0), ("gQ", 0),
-    ("beta", 0, 1), ("gQ", 2), ("gQ", 3), ("xQ", 6), ("beta", 1, 1), ("xQ", 7), ("mm", 6, 0), ("hs", 0, 0, 0),
-    ("es", 0, 1), ("mm", 0, 1), ("hs", 0, 0, 1), ("beta", 0, 0), ("tanh", 1, 1), ("mm", 7, 0), ("mm", 3, 1),
-    ("hT", 0, 0, 0), ("tanh", 4, 0), ("sq", 0, 0, 3), ("es", 0, 0), ("tanh", 6, 0), ("tanh", 0, 1),
-    ("mm", 2, 1), ("mm", 4, 1), ("tanh", 7, 0), ("hQ", 0, 0, 1), ("hT", 0, 1, 1), ("tanh", 3, 1),
-    ("beta", 0, 2), ("beta", 0, 3), ("mm", 7, 1), ("hQ", 0, 0, 0), ("sq", 0, 0, 1), ("es", 1, 1),
-    ("tanh", 2, 1), ("sq", 0, 0, 0), ("hs", 0, 1, 0), ("sq", 0, 0, 2), ("tanh", 4, 1), ("sq", 0, 1, 1),
-    ("hs", 0, 1, 1), ("hT", 1, 0, 3), ("hT", 1, 0, 2), ("hT", 0, 1, 2), ("es", 0, 2), ("tanh", 7, 1),
-    ("hT", 0, 1, 3), ("sq", 1, 0, 2), ("mm", 6, 1), ("es", 0, 3), ("hs", 1, 0, 0), ("sq", 1, 0, 3),
-    ("beta", 1, 2), ("beta", 1, 3), ("eQ", 0), ("mm", 5, 1), ("beta", 1, 0), ("es", 1, 2), ("es", 1, 3),
-    ("tanh", 6, 1), ("hT", 1, 0, 1), ("sq", 0, 1, 3), ("sq", 0, 1, 2), ("hQ", 0, 1, 0), ("hT", 0, 1, 0),
-    ("tanh", 5, 1), ("es", 1, 0), ("hQ", 0, 1, 1), ("sq", 1, 0, 1), ("hT", 1, 0, 0), ("eQ", 1), ("c0", 0, 2),
-    ("c0", 0, 3), ("hT", 1, 1, 1), ("c1", 0, 2), ("sq", 0, 1, 0), ("hs", 1, 0, 1), ("c1", 0, 3),
-    ("hT", 1, 1, 0), ("rec", 0), ("hs", 1, 1, 0), ("hT", 1, 1, 2), ("sq", 1, 0, 0), ("csq", 0, 2),
-    ("hT", 1, 1, 3), ("c0", 0, 1), ("c0", 0, 0), ("csq", 0, 3), ("sq", 1, 1, 1), ("hs", 1, 1, 1),
-    ("hQ", 1, 0, 0), ("c1", 0, 1), ("sq", 1, 1, 2), ("csq", 0, 1), ("hQ", 1, 1, 0), ("hQ", 1, 0, 1),
-    ("c1", 0, 0), ("out", 0, 3), ("csq", 0, 0), ("c0", 1, 1), ("c1", 1, 1), ("sq", 1, 1, 3), ("c0", 1, 2),
-    ("sq", 1, 1, 0), ("csq", 1, 1), ("hQ", 1, 1, 1), ("out", 0, 1), ("c1", 1, 2), ("c0", 1, 0), ("out", 0, 0),
-    ("rec", 1), ("c1", 1, 0), ("out", 0, 2), ("c0", 1, 3), ("csq", 1, 2), ("c1", 1, 3), ("out", 1, 2),
-    ("csq", 1, 0), ("out", 1, 1), ("out", 1, 0), ("csq", 1, 3), ("out", 1, 3),
+    ("castV", 0, 0), ("castS", 1, 0), ("castS", 3, 0), ("xT", 0, 0), ("castV", 1, 1), ("castS", 0, 1),
+    ("xE", 0, 0), ("xT", 1, 0), ("xT", 1, 1), ("xT", 3, 0), ("xE", 1, 0), ("castS", 2, 0), ("castS", 2, 1),
+    ("xT", 0, 1), ("castS", 3, 1), ("xE", 1, 1), ("xT", 2, 0), ("xE", 0, 1), ("xQ", 1), ("xT", 2, 1),
+    ("xT", 3, 1), ("xQ", 0), ("castS", 5, 0), ("xE", 2, 1), ("castS", 7, 1), ("castS", 6, 0), ("xE", 3, 0),
+    ("castS", 6, 1), ("xE", 3, 1), ("xE", 2, 0), ("mm", 0, 0), ("mm", 1, 0), ("xT", 6, 0), ("xQ", 3),
+    ("castS", 5, 1), ("xT", 6, 1), ("xE", 6, 0), ("xT", 5, 0), ("castS", 4, 0), ("xT", 5, 1), ("gT", 1),
+    ("castS", 7, 0), ("tanh", 1, 0), ("tanh", 0, 0), ("gT", 0), ("gE", 1), ("xE", 6, 1), ("xE", 5, 0),
+    ("xT", 4, 0), ("xQ", 2), ("castS", 4, 1), ("mm", 2, 0), ("xE", 5, 1), ("mm", 3, 0), ("gE", 0), ("xE", 4, 0),
+    ("xT", 7, 0), ("xT", 4, 1), ("gT", 3), ("gQ", 1), ("gT", 2), ("xQ", 5), ("xQ", 6), ("tanh", 2, 0),
+    ("xT", 7, 1), ("tanh", 3, 0), ("hT", 0, 0, 2), ("mm", 5, 0), ("gQ", 0), ("mm", 1, 1), ("gE", 3),
+    ("xE", 4, 1), ("hq", 0, 0, 1), ("tanh", 5, 0), ("xE", 7, 0), ("xQ", 4), ("tanh", 1, 1), ("gE", 2),
+    ("beta", 0, 0), ("beta", 0, 1), ("xE", 7, 1), ("mm", 4, 0), ("mm", 6, 0), ("hT", 0, 0, 3), ("tanh", 4, 0),
+    ("mm", 0, 1), ("gQ", 3), ("hq", 0, 0, 0), ("xQ", 7), ("mm", 7, 0), ("tanh", 6, 0), ("es", 0, 0),
+    ("tanh", 0, 1), ("tanh", 7, 0), ("beta", 0, 3), ("gQ", 2), ("beta", 1, 1), ("sq", 0, 0, 2), ("mm", 3, 1),
+    ("mm", 2, 1), ("hT", 0, 1, 1), ("hT", 0, 0, 0), ("tanh", 3, 1), ("hT", 0, 0, 1), ("es", 0, 1),
+    ("hq", 0, 0, 2), ("beta", 0, 2), ("beta", 1, 2), ("hq", 0, 0, 3), ("hQ", 0, 0, 0), ("sq", 0, 0, 3),
+    ("tanh", 2, 1), ("mm", 7, 1), ("es", 0, 3), ("hT", 1, 0, 2), ("hq", 0, 1, 0), ("sq", 0, 1, 1), ("es", 1, 1),
+    ("hq", 0, 1, 1), ("hq", 0, 1, 3), ("es", 0, 2), ("hT", 0, 1, 3), ("es", 1, 2), ("mm", 4, 1), ("beta", 1, 0),
+    ("hT", 1, 0, 0), ("hq", 0, 1, 2), ("hq", 1, 0, 0), ("hT", 1, 0, 1), ("beta", 1, 3), ("sq", 0, 0, 1),
+    ("eQ", 0), ("mm", 5, 1), ("hQ", 0, 0, 1), ("hq", 1, 0, 1), ("sq", 0, 0, 0), ("mm", 6, 1), ("es", 1, 0),
+    ("hT", 1, 0, 3), ("c0", 0, 3), ("hQ", 0, 1, 0), ("tanh", 7, 1), ("hT", 0, 1, 0), ("sq", 0, 1, 3),
+    ("sq", 1, 0, 2), ("tanh", 4, 1), ("sq", 1, 0, 0), ("sq", 1, 0, 1), ("tanh", 5, 1), ("es", 1, 3),
+    ("hT", 0, 1, 2), ("hQ", 0, 1, 1), ("eQ", 1), ("c1", 0, 3), ("c0", 0, 2), ("tanh", 6, 1), ("hT", 1, 1, 2),
+    ("c1", 0, 2), ("hq", 1, 1, 0), ("c0", 0, 1), ("sq", 1, 0, 3), ("hq", 1, 0, 3), ("hq", 1, 1, 3),
+    ("hq", 1, 1, 2), ("hT", 1, 1, 0), ("sq", 0, 1, 0), ("c1", 0, 1), ("csq", 0, 3), ("sq", 0, 1, 2),
+    ("csq", 0, 2), ("hq", 1, 1, 1), ("hQ", 1, 1, 1), ("hq", 1, 0, 2), ("sq", 1, 1, 2), ("c0", 0, 0),
+    ("hT", 1, 1, 3), ("hQ", 1, 0, 0), ("c1", 0, 0), ("hQ", 1, 1, 0), ("csq", 0, 1), ("rec", 0), ("hQ", 1, 0, 1),
+    ("out", 0, 1), ("sq", 1, 1, 0), ("csq", 0, 0), ("hT", 1, 1, 1), ("c0", 1, 1), ("c1", 1, 1), ("sq", 1, 1, 1),
+    ("out", 0, 2), ("c0", 1, 2), ("sq", 1, 1, 3), ("csq", 1, 1), ("c1", 1, 2), ("c0", 1, 0), ("c0", 1, 3),
+    ("rec", 1), ("csq", 1, 2), ("c1", 1, 0), ("out", 0, 0), ("c1", 1, 3), ("csq", 1, 0), ("csq", 1, 3),
+    ("out", 1, 1), ("out", 1, 2), ("out", 0, 3), ("out", 1, 0), ("out", 1, 3),
 ]
 
 
@@ -220,14 +221,20 @@ def tile_stochasticconfigurationcandidatescores_w4_kernel(
                 out=junk[:], in_=banks["h", f, gi, fb][:], func=ACT.Square, accum_out=part[f][:, fb, gi : gi + 1]
             )
 
-        def hs(f, gi, half):
-            sl = slice(half * 256, (half + 1) * 256)
-            nc.vector.tensor_tensor(
+        def hs(eng, f, gi, qu):
+            sl = slice(qu * P, (qu + 1) * P)
+            eng.tensor_tensor(
                 out=hsb[f, gi][:, sl, :].rearrange("p (c i) t -> p c t i", i=4),
                 in0=hh[f, gi][:, :, sl].rearrange("p t (c i) -> p c t i", i=4),
-                in1=s4[:, gi, :].unsqueeze(1).unsqueeze(3).to_broadcast([P, 64, 4, 4]),
+                in1=s4[:, gi, :].unsqueeze(1).unsqueeze(3).to_broadcast([P, 32, 4, 4]),
                 op=ALU.mult,
             )
+
+        def h_v(f, gi, qu):
+            hs(nc.vector, f, gi, qu)
+
+        def h_g(f, gi, qu):
+            hs(nc.gpsimd, f, gi, qu)
 
         def h_q(f, gi, half):
             sl = slice(half * 256, (half + 1) * 256)
@@ -273,9 +280,14 @@ def tile_stochasticconfigurationcandidatescores_w4_kernel(
         STEP = {
             "castS": cast_s, "castV": cast_v, "xT": x_t, "xE": x_e, "xQ": x_q, "mm": mm, "tanh": tanh,
             "gT": g_t, "gE": g_e, "gQ": g_q, "beta": beta, "es": e_s, "eQ": e_q, "hT": h_t, "sq": sq,
-            "hs": hs, "hQ": h_q, "rec": rec, "c0": c0, "c1": c1, "csq": c_sq, "out": o,
+            "hq": h_v, "hG": h_g, "hQ": h_q, "rec": rec, "c0": c0, "c1": c1, "csq": c_sq, "out": o,
         }
 
+        wz = kt("wz", [P, 512], BF16)
+        nc.vector.memset(wz[:], 0.0)
+        wb = bank("ec", "warm", EC)
+        for i in range(5):
+            nc.tensor.matmul(wb[:], wz[:, 0:P], wz[:], start=True, stop=True)
         make_identity(nc, ident[:])
         nc.vector.memset(warm[:], 0.0)
         nc.scalar.activation(out=warm[:, 1:2], in_=warm[:, 0:1], func=ACT.Tanh)
@@ -289,35 +301,34 @@ def tile_stochasticconfigurationcandidatescores_w4_kernel(
             r0 = sum(X_LOADS[:h])
             ld(out=xs[h][:], in_=xv[r0 // 4][:, r0 % 4 : r0 % 4 + X_LOADS[h], :])
 
+        wv = w_words.rearrange("g p n -> p g n")
+        gv = g.rearrange("(g p t) k -> g p t k", p=P, t=4)
+        tv = t.rearrange("(g p t) k -> g p t k", p=P, t=4)
         ldx(0)
         ldx(1)
         ld(out=xsc[:], in_=x_scale.rearrange("o (g p t) -> p (o g) t", p=P, t=4))
         ldx(2)
+        ld(out=wwd[0][:].bitcast(I32), in_=wv[:, :, 0:1024].bitcast(I32))
         for qd in range(4):
             ld(
                 out=wsc[32 * qd : 32 * qd + 4, :, :].bitcast(I32),
                 in_=w_scales[:, 4 * qd : 4 * qd + 4, :].rearrange("g r n -> r g n").bitcast(I32),
             )
-        wv = w_words.rearrange("g p n -> p g n")
-        ld(out=wwd[0][:].bitcast(I32), in_=wv[:, :, 0:1024].bitcast(I32))
-        for h in range(3, len(X_LOADS)):
-            ldx(h)
+        ldx(3)
         ld(out=s4[:], in_=s.rearrange("(g p t) -> p g t", p=P, t=4))
+        ld(out=gs[0][:], in_=gv[0])
         ld(out=wwd[1][:].bitcast(I32), in_=wv[:, :, 1024:2048].bitcast(I32))
+        ld(out=bwd[:].bitcast(I32), in_=beta_words[0].bitcast(I32))
         for qd in range(4):
             ld(
                 out=bsc[32 * qd : 32 * qd + 4, :].bitcast(I32),
                 in_=beta_scales[0][4 * qd : 4 * qd + 4, :].bitcast(I32),
             )
-        ld(out=bwd[:].bitcast(I32), in_=beta_words[0].bitcast(I32))
-        gv = g.rearrange("(g p t) k -> g p t k", p=P, t=4)
-        tv = t.rearrange("(g p t) k -> g p t k", p=P, t=4)
-        ld(out=gs[0][:], in_=gv[0])
-        ld(out=ts[0][:], in_=tv[0])
         ld(out=gs[1][:], in_=gv[1])
+        ld(out=ts[0][:], in_=tv[0])
         ld(out=ts[1][:], in_=tv[1])
         ld(out=taub[:], in_=tau.partition_broadcast(P))
 
-        with tc.manual_schedule(engines={mybir.EngineType.PE, mybir.EngineType.Activation, mybir.EngineType.DVE}):
+        with tc.manual_schedule():
             for st in ORDER:
                 STEP[st[0]](*st[1:])

@@ -18,39 +18,39 @@ N, D, F, L, Q = 1024, 1024, 1024, 512, 512
 FLOPS = 2 * N * D * F + 2 * N * L * Q + 2 * N * F * Q
 P = 128
 X_LOADS = [1, 1, 2, 4]
-TR, MM, EC = 4, 2, 2
+TR, MM, EC = 3, 2, 3
 ORDER = [
-    ("castV", 0, 0), ("castS", 1, 0), ("castS", 3, 0), ("xT", 0, 0), ("castV", 1, 1), ("castS", 0, 1),
-    ("xE", 0, 0), ("xT", 1, 0), ("xT", 1, 1), ("xT", 3, 0), ("xE", 1, 0), ("castS", 2, 0), ("castS", 2, 1),
-    ("xT", 0, 1), ("castS", 3, 1), ("xE", 1, 1), ("xT", 2, 0), ("xE", 0, 1), ("xQ", 1), ("xT", 2, 1),
-    ("xT", 3, 1), ("xQ", 0), ("castS", 5, 0), ("xE", 2, 1), ("castS", 7, 1), ("castS", 6, 0), ("xE", 3, 0),
-    ("castS", 6, 1), ("xE", 3, 1), ("xE", 2, 0), ("mm", 0, 0), ("mm", 1, 0), ("xT", 6, 0), ("xQ", 3),
-    ("castS", 5, 1), ("xT", 6, 1), ("xE", 6, 0), ("xT", 5, 0), ("castS", 4, 0), ("xT", 5, 1), ("gT", 1),
-    ("castS", 7, 0), ("tanh", 1, 0), ("tanh", 0, 0), ("gT", 0), ("gE", 1), ("xE", 6, 1), ("xE", 5, 0),
-    ("xT", 4, 0), ("xQ", 2), ("castS", 4, 1), ("mm", 2, 0), ("xE", 5, 1), ("mm", 3, 0), ("gE", 0), ("xE", 4, 0),
-    ("xT", 7, 0), ("xT", 4, 1), ("gT", 3), ("gQ", 1), ("gT", 2), ("xQ", 5), ("xQ", 6), ("tanh", 2, 0),
-    ("xT", 7, 1), ("tanh", 3, 0), ("hT", 0, 0, 2), ("mm", 5, 0), ("gQ", 0), ("mm", 1, 1), ("gE", 3),
-    ("xE", 4, 1), ("hq", 0, 0, 1), ("tanh", 5, 0), ("xE", 7, 0), ("xQ", 4), ("tanh", 1, 1), ("gE", 2),
-    ("beta", 0, 0), ("beta", 0, 1), ("xE", 7, 1), ("mm", 4, 0), ("mm", 6, 0), ("hT", 0, 0, 3), ("tanh", 4, 0),
-    ("mm", 0, 1), ("gQ", 3), ("hq", 0, 0, 0), ("xQ", 7), ("mm", 7, 0), ("tanh", 6, 0), ("es", 0, 0),
-    ("tanh", 0, 1), ("tanh", 7, 0), ("beta", 0, 3), ("gQ", 2), ("beta", 1, 1), ("sq", 0, 0, 2), ("mm", 3, 1),
-    ("mm", 2, 1), ("hT", 0, 1, 1), ("hT", 0, 0, 0), ("tanh", 3, 1), ("hT", 0, 0, 1), ("es", 0, 1),
-    ("hq", 0, 0, 2), ("beta", 0, 2), ("beta", 1, 2), ("hq", 0, 0, 3), ("hQ", 0, 0, 0), ("sq", 0, 0, 3),
-    ("tanh", 2, 1), ("mm", 7, 1), ("es", 0, 3), ("hT", 1, 0, 2), ("hq", 0, 1, 0), ("sq", 0, 1, 1), ("es", 1, 1),
-    ("hq", 0, 1, 1), ("hq", 0, 1, 3), ("es", 0, 2), ("hT", 0, 1, 3), ("es", 1, 2), ("mm", 4, 1), ("beta", 1, 0),
-    ("hT", 1, 0, 0), ("hq", 0, 1, 2), ("hq", 1, 0, 0), ("hT", 1, 0, 1), ("beta", 1, 3), ("sq", 0, 0, 1),
-    ("eQ", 0), ("mm", 5, 1), ("hQ", 0, 0, 1), ("hq", 1, 0, 1), ("sq", 0, 0, 0), ("mm", 6, 1), ("es", 1, 0),
-    ("hT", 1, 0, 3), ("c0", 0, 3), ("hQ", 0, 1, 0), ("tanh", 7, 1), ("hT", 0, 1, 0), ("sq", 0, 1, 3),
-    ("sq", 1, 0, 2), ("tanh", 4, 1), ("sq", 1, 0, 0), ("sq", 1, 0, 1), ("tanh", 5, 1), ("es", 1, 3),
-    ("hT", 0, 1, 2), ("hQ", 0, 1, 1), ("eQ", 1), ("c1", 0, 3), ("c0", 0, 2), ("tanh", 6, 1), ("hT", 1, 1, 2),
-    ("c1", 0, 2), ("hq", 1, 1, 0), ("c0", 0, 1), ("sq", 1, 0, 3), ("hq", 1, 0, 3), ("hq", 1, 1, 3),
-    ("hq", 1, 1, 2), ("hT", 1, 1, 0), ("sq", 0, 1, 0), ("c1", 0, 1), ("csq", 0, 3), ("sq", 0, 1, 2),
-    ("csq", 0, 2), ("hq", 1, 1, 1), ("hQ", 1, 1, 1), ("hq", 1, 0, 2), ("sq", 1, 1, 2), ("c0", 0, 0),
-    ("hT", 1, 1, 3), ("hQ", 1, 0, 0), ("c1", 0, 0), ("hQ", 1, 1, 0), ("csq", 0, 1), ("rec", 0), ("hQ", 1, 0, 1),
-    ("out", 0, 1), ("sq", 1, 1, 0), ("csq", 0, 0), ("hT", 1, 1, 1), ("c0", 1, 1), ("c1", 1, 1), ("sq", 1, 1, 1),
-    ("out", 0, 2), ("c0", 1, 2), ("sq", 1, 1, 3), ("csq", 1, 1), ("c1", 1, 2), ("c0", 1, 0), ("c0", 1, 3),
-    ("rec", 1), ("csq", 1, 2), ("c1", 1, 0), ("out", 0, 0), ("c1", 1, 3), ("csq", 1, 0), ("csq", 1, 3),
-    ("out", 1, 1), ("out", 1, 2), ("out", 0, 3), ("out", 1, 0), ("out", 1, 3),
+    ("castV", 0, 0), ("castV", 0, 1), ("castS", 1, 0), ("castV", 1, 1), ("xT", 0, 0), ("xT", 0, 1),
+    ("castS", 2, 0), ("castS", 2, 1), ("xT", 1, 0), ("xT", 1, 1), ("xE", 0, 0), ("xE", 0, 1), ("castS", 3, 0),
+    ("castS", 3, 1), ("xT", 2, 0), ("xT", 2, 1), ("xE", 1, 0), ("xQ", 0), ("xE", 1, 1), ("castS", 4, 0),
+    ("castS", 4, 1), ("xT", 3, 0), ("xT", 3, 1), ("xE", 2, 0), ("xQ", 1), ("xE", 2, 1), ("mm", 0, 0),
+    ("tanh", 0, 0), ("castS", 5, 0), ("castS", 5, 1), ("xT", 4, 0), ("xT", 4, 1), ("xE", 3, 0), ("xQ", 2),
+    ("xE", 3, 1), ("mm", 1, 0), ("tanh", 1, 0), ("castS", 6, 0), ("castS", 6, 1), ("xT", 5, 0), ("xT", 5, 1),
+    ("xE", 4, 0), ("xQ", 3), ("xE", 4, 1), ("mm", 2, 0), ("tanh", 2, 0), ("mm", 0, 1), ("tanh", 0, 1),
+    ("castS", 7, 0), ("castS", 7, 1), ("xT", 6, 0), ("xT", 6, 1), ("gT", 0), ("gE", 0), ("xE", 5, 0), ("xQ", 4),
+    ("xE", 5, 1), ("mm", 3, 0), ("tanh", 3, 0), ("mm", 1, 1), ("tanh", 1, 1), ("xT", 7, 0), ("xT", 7, 1),
+    ("gT", 1), ("gE", 1), ("xE", 6, 0), ("xQ", 5), ("xE", 6, 1), ("mm", 4, 0), ("tanh", 4, 0), ("gQ", 0),
+    ("gT", 2), ("gE", 2), ("xE", 7, 0), ("xQ", 6), ("xE", 7, 1), ("mm", 5, 0), ("tanh", 5, 0), ("gQ", 1),
+    ("hq", 0, 0, 0), ("gT", 3), ("gE", 3), ("xQ", 7), ("mm", 6, 0), ("tanh", 6, 0), ("gQ", 2), ("hq", 0, 0, 1),
+    ("mm", 7, 0), ("tanh", 7, 0), ("beta", 0, 0), ("beta", 0, 1), ("mm", 2, 1), ("mm", 3, 1), ("beta", 0, 2),
+    ("beta", 0, 3), ("tanh", 2, 1), ("tanh", 3, 1), ("hT", 0, 0, 0), ("hT", 0, 0, 1), ("hq", 0, 0, 2),
+    ("gQ", 3), ("es", 0, 0), ("hq", 0, 0, 3), ("es", 0, 1), ("sq", 0, 0, 0), ("sq", 0, 0, 1), ("hQ", 0, 0, 0),
+    ("mm", 4, 1), ("mm", 5, 1), ("beta", 1, 0), ("beta", 1, 1), ("tanh", 4, 1), ("tanh", 5, 1), ("hT", 0, 0, 2),
+    ("hT", 0, 0, 3), ("hq", 0, 1, 0), ("es", 0, 2), ("hq", 0, 1, 1), ("es", 0, 3), ("sq", 0, 0, 2),
+    ("sq", 0, 0, 3), ("hQ", 0, 0, 1), ("mm", 6, 1), ("mm", 7, 1), ("beta", 1, 2), ("beta", 1, 3),
+    ("tanh", 6, 1), ("tanh", 7, 1), ("hT", 0, 1, 0), ("hT", 0, 1, 1), ("hq", 0, 1, 2), ("es", 1, 0),
+    ("hq", 0, 1, 3), ("es", 1, 1), ("sq", 0, 1, 0), ("sq", 0, 1, 1), ("hQ", 0, 1, 0), ("eQ", 0),
+    ("hT", 0, 1, 2), ("hT", 0, 1, 3), ("es", 1, 2), ("es", 1, 3), ("sq", 0, 1, 2), ("sq", 0, 1, 3),
+    ("hQ", 0, 1, 1), ("eQ", 1), ("hT", 1, 0, 0), ("hT", 1, 0, 1), ("hq", 1, 0, 0), ("hq", 1, 0, 1),
+    ("sq", 1, 0, 0), ("sq", 1, 0, 1), ("hT", 1, 0, 2), ("hT", 1, 0, 3), ("hq", 1, 0, 2), ("rec", 0),
+    ("hq", 1, 0, 3), ("hQ", 1, 0, 0), ("sq", 1, 0, 2), ("sq", 1, 0, 3), ("hT", 1, 1, 0), ("hT", 1, 1, 1),
+    ("c0", 0, 0), ("c1", 0, 0), ("c0", 0, 1), ("c1", 0, 1), ("hq", 1, 1, 0), ("hq", 1, 1, 1), ("hQ", 1, 0, 1),
+    ("sq", 1, 1, 0), ("sq", 1, 1, 1), ("csq", 0, 0), ("csq", 0, 1), ("hT", 1, 1, 2), ("hT", 1, 1, 3),
+    ("c0", 0, 2), ("c1", 0, 2), ("c0", 0, 3), ("c1", 0, 3), ("hq", 1, 1, 2), ("hq", 1, 1, 3), ("hQ", 1, 1, 0),
+    ("sq", 1, 1, 2), ("sq", 1, 1, 3), ("csq", 0, 2), ("csq", 0, 3), ("out", 0, 0), ("out", 0, 1),
+    ("hQ", 1, 1, 1), ("c0", 1, 0), ("c1", 1, 0), ("csq", 1, 0), ("out", 0, 2), ("c0", 1, 1), ("c1", 1, 1),
+    ("csq", 1, 1), ("rec", 1), ("out", 0, 3), ("c0", 1, 2), ("c1", 1, 2), ("csq", 1, 2), ("out", 1, 0),
+    ("c0", 1, 3), ("c1", 1, 3), ("csq", 1, 3), ("out", 1, 1), ("out", 1, 2), ("out", 1, 3),
 ]
 
 
@@ -200,9 +200,9 @@ def tile_stochasticconfigurationcandidatescores_w4_kernel(
 
         def e_s(gi, qb):
             nc.vector.tensor_tensor(
-                out=eb[gi][:, qb * P : (qb + 1) * P, :],
-                in0=ts[gi][:, :, qb * P : (qb + 1) * P].rearrange("p t q -> p q t"),
-                in1=banks["b", gi, qb][:].rearrange("p (t q) -> p q t", t=4),
+                out=eb[gi][:, qb * P : (qb + 1) * P, :].rearrange("p (c i) t -> p c t i", i=4),
+                in0=ts[gi][:, :, qb * P : (qb + 1) * P].rearrange("p t (c i) -> p c t i", i=4),
+                in1=banks["b", gi, qb][:].rearrange("p (t c i) -> p c t i", t=4, i=4),
                 op=ALU.subtract,
             )
 

@@ -16,319 +16,387 @@ ALU = mybir.AluOpType
 
 N, D, F, L, Q = 1024, 1024, 1024, 512, 512
 FLOPS = 2 * N * D * F + 2 * N * L * Q + 2 * N * F * Q
+
 P = 128
-X_LOADS = [1, 1, 2, 4]
-TR, MM, EC = 3, 2, 3
-ORDER = [
-    ("castV", 0, 0), ("castV", 0, 1), ("castS", 1, 0), ("castV", 1, 1), ("xT", 0, 0), ("xT", 0, 1),
-    ("castS", 2, 0), ("castS", 2, 1), ("xT", 1, 0), ("xT", 1, 1), ("xE", 0, 0), ("xE", 0, 1), ("castS", 3, 0),
-    ("castS", 3, 1), ("xT", 2, 0), ("xT", 2, 1), ("xE", 1, 0), ("xQ", 0), ("xE", 1, 1), ("castS", 4, 0),
-    ("castS", 4, 1), ("xT", 3, 0), ("xT", 3, 1), ("xE", 2, 0), ("xQ", 1), ("xE", 2, 1), ("mm", 0, 0),
-    ("tanh", 0, 0), ("castS", 5, 0), ("castS", 5, 1), ("xT", 4, 0), ("xT", 4, 1), ("xE", 3, 0), ("xQ", 2),
-    ("xE", 3, 1), ("mm", 1, 0), ("tanh", 1, 0), ("castS", 6, 0), ("castS", 6, 1), ("xT", 5, 0), ("xT", 5, 1),
-    ("xE", 4, 0), ("xQ", 3), ("xE", 4, 1), ("mm", 2, 0), ("tanh", 2, 0), ("mm", 0, 1), ("tanh", 0, 1),
-    ("castS", 7, 0), ("castS", 7, 1), ("xT", 6, 0), ("xT", 6, 1), ("gT", 0), ("gE", 0), ("xE", 5, 0), ("xQ", 4),
-    ("xE", 5, 1), ("mm", 3, 0), ("tanh", 3, 0), ("mm", 1, 1), ("tanh", 1, 1), ("xT", 7, 0), ("xT", 7, 1),
-    ("gT", 1), ("gE", 1), ("xE", 6, 0), ("xQ", 5), ("xE", 6, 1), ("mm", 4, 0), ("tanh", 4, 0), ("gQ", 0),
-    ("gT", 2), ("gE", 2), ("xE", 7, 0), ("xQ", 6), ("xE", 7, 1), ("mm", 5, 0), ("tanh", 5, 0), ("gQ", 1),
-    ("hq", 0, 0, 0), ("gT", 3), ("gE", 3), ("xQ", 7), ("mm", 6, 0), ("tanh", 6, 0), ("gQ", 2), ("hq", 0, 0, 1),
-    ("mm", 7, 0), ("tanh", 7, 0), ("beta", 0, 0), ("beta", 0, 1), ("mm", 2, 1), ("mm", 3, 1), ("beta", 0, 2),
-    ("beta", 0, 3), ("tanh", 2, 1), ("tanh", 3, 1), ("hT", 0, 0, 0), ("hT", 0, 0, 1), ("hq", 0, 0, 2),
-    ("gQ", 3), ("es", 0, 0), ("hq", 0, 0, 3), ("es", 0, 1), ("sq", 0, 0, 0), ("sq", 0, 0, 1), ("hQ", 0, 0, 0),
-    ("mm", 4, 1), ("mm", 5, 1), ("beta", 1, 0), ("beta", 1, 1), ("tanh", 4, 1), ("tanh", 5, 1), ("hT", 0, 0, 2),
-    ("hT", 0, 0, 3), ("hq", 0, 1, 0), ("es", 0, 2), ("hq", 0, 1, 1), ("es", 0, 3), ("sq", 0, 0, 2),
-    ("sq", 0, 0, 3), ("hQ", 0, 0, 1), ("mm", 6, 1), ("mm", 7, 1), ("beta", 1, 2), ("beta", 1, 3),
-    ("tanh", 6, 1), ("tanh", 7, 1), ("hT", 0, 1, 0), ("hT", 0, 1, 1), ("hq", 0, 1, 2), ("es", 1, 0),
-    ("hq", 0, 1, 3), ("es", 1, 1), ("sq", 0, 1, 0), ("sq", 0, 1, 1), ("hQ", 0, 1, 0), ("eQ", 0),
-    ("hT", 0, 1, 2), ("hT", 0, 1, 3), ("es", 1, 2), ("es", 1, 3), ("sq", 0, 1, 2), ("sq", 0, 1, 3),
-    ("hQ", 0, 1, 1), ("eQ", 1), ("hT", 1, 0, 0), ("hT", 1, 0, 1), ("hq", 1, 0, 0), ("hq", 1, 0, 1),
-    ("sq", 1, 0, 0), ("sq", 1, 0, 1), ("hT", 1, 0, 2), ("hT", 1, 0, 3), ("hq", 1, 0, 2), ("rec", 0),
-    ("hq", 1, 0, 3), ("hQ", 1, 0, 0), ("sq", 1, 0, 2), ("sq", 1, 0, 3), ("hT", 1, 1, 0), ("hT", 1, 1, 1),
-    ("c0", 0, 0), ("c1", 0, 0), ("c0", 0, 1), ("c1", 0, 1), ("hq", 1, 1, 0), ("hq", 1, 1, 1), ("hQ", 1, 0, 1),
-    ("sq", 1, 1, 0), ("sq", 1, 1, 1), ("csq", 0, 0), ("csq", 0, 1), ("hT", 1, 1, 2), ("hT", 1, 1, 3),
-    ("c0", 0, 2), ("c1", 0, 2), ("c0", 0, 3), ("c1", 0, 3), ("hq", 1, 1, 2), ("hq", 1, 1, 3), ("hQ", 1, 1, 0),
-    ("sq", 1, 1, 2), ("sq", 1, 1, 3), ("csq", 0, 2), ("csq", 0, 3), ("out", 0, 0), ("out", 0, 1),
-    ("hQ", 1, 1, 1), ("c0", 1, 0), ("c1", 1, 0), ("csq", 1, 0), ("out", 0, 2), ("c0", 1, 1), ("c1", 1, 1),
-    ("csq", 1, 1), ("rec", 1), ("out", 0, 3), ("c0", 1, 2), ("c1", 1, 2), ("csq", 1, 2), ("out", 1, 0),
-    ("c0", 1, 3), ("c1", 1, 3), ("csq", 1, 3), ("out", 1, 1), ("out", 1, 2), ("out", 1, 3),
-]
+J = 4
+BANK = 512
+ROW_TILES = N // P
+NODE_HALF = F // 2
+FP4_BYTES = 2
+
+X_LOADS = (1, 1, 2, 4)
+SINGLE_ROW_TILES = 4
+WARM_UP_MATMULS = 5
+LAST_BLOCK_PARTS = 2
+
+TURNED_BANKS = 4
+PREACT_BANKS = 2
+PRODUCT_BANKS = 2
 
 
 def tile_stochasticconfigurationcandidatescores_w4_kernel(
-    tc, x_bytes, x_scale, w_words, w_scales, s, t, g, beta_words, beta_scales, tau, out
+    tc, x_bytes, x_scale, w_words, w_scales, gain, target, hidden, beta_words, beta_scales, tau, out
 ):
     nc = tc.nc
     with ExitStack() as ctx:
         keep = ctx.enter_context(tc.tile_pool(name="keep", bufs=1))
         psum = ctx.enter_context(tc.psum_pool(name="psum", bufs=1))
 
-        def kt(name, shape, dt):
-            return keep.tile(shape, dt, name=name, align_bytes=64)
+        def sbuf(name, shape, dtype):
+            return keep.tile(shape, dtype, name=name, align_bytes=64)
 
-        ident = kt("ident", [P, P], F32)
-        warm = kt("warm", [P, 2], F32)
-        xs = [kt("xs%d" % h, [P, n, D], U8) for h, n in enumerate(X_LOADS)]
-        xrow = {}
-        for h, n in enumerate(X_LOADS):
-            for i in range(n):
-                xrow[sum(X_LOADS[:h]) + i] = (h, i)
-        xb = [kt("xb%d" % r, [P, D], BF16) for r in range(8)]
-        xsc = kt("xsc", [P, 2, 4], F32)
-        xg = [kt("xg%d" % r, [P, 2, P, 4], BF16) for r in range(8)]
-        xcod = [kt("xcod%d" % r, [P, 2, P], U32) for r in range(8)]
-        xcsc = [kt("xcsc%d" % r, [P, 2, P], U8) for r in range(8)]
-        wwd = [kt("wwd%d" % h, [P, 2, 1024], U8) for h in range(2)]
-        wsc = kt("wsc", [P, 2, F], U8)
-        bwd = kt("bwd", [P, 2 * Q], U8)
-        bsc = kt("bsc", [P, Q], U8)
-        gs = [kt("gs%d" % h, [P, 4, L], BF16) for h in range(2)]
-        gg = [kt("gg%d" % j, [P, 2, P, 4], BF16) for j in range(4)]
-        gcod = [kt("gcod%d" % j, [P, 2, P], U32) for j in range(4)]
-        gcsc = [kt("gcsc%d" % j, [P, 2, P], U8) for j in range(4)]
-        ts = [kt("ts%d" % h, [P, 4, Q], BF16) for h in range(2)]
-        s4 = kt("s4", [P, 2, 4], BF16)
-        taub = kt("taub", [P, Q], BF16)
-        eb = [kt("eb%d" % h, [P, Q, 4], BF16) for h in range(2)]
-        ecod = [kt("ecod%d" % h, [P, Q], U32) for h in range(2)]
-        ecsc = [kt("ecsc%d" % h, [P, Q], U8) for h in range(2)]
-        hh = {}
-        hsb = {}
-        hcod = {}
-        hcsc = {}
-        for f in range(2):
-            for gi in range(2):
-                hh[f, gi] = kt("h%d%d" % (f, gi), [P, 4, 512], F32)
-                hsb[f, gi] = kt("hs%d%d" % (f, gi), [P, 512, 4], BF16)
-                hcod[f, gi] = kt("hcod%d%d" % (f, gi), [P, 512], U32)
-                hcsc[f, gi] = kt("hcsc%d%d" % (f, gi), [P, 512], U8)
-        part = [kt("part%d" % f, [P, 4, 2], F32) for f in range(2)]
-        hsum = [kt("hsum%d" % f, [P, 4], F32) for f in range(2)]
-        rinv = [kt("rinv%d" % f, [P, 4], F32) for f in range(2)]
-        junk = kt("junk", [P, 512], BF16)
-        csqs = [kt("csq%d" % i, [P, Q], F32) for i in range(8)]
-        outs = [kt("out%d" % i, [P, Q], F32) for i in range(8)]
+        x_raw = [sbuf("x_raw%d" % i, [P, n, D], U8) for i, n in enumerate(X_LOADS)]
+        x_scl = sbuf("x_scl", [P, 2, J], F32)
+        w_wrd = [sbuf("w_wrd%d" % b, [P, 2, FP4_BYTES * NODE_HALF], U8) for b in range(2)]
+        w_scl = sbuf("w_scl", [P, 2, F], U8)
+        b_wrd = sbuf("b_wrd", [P, FP4_BYTES * Q], U8)
+        b_scl = sbuf("b_scl", [P, Q], U8)
+        hid = [sbuf("hid%d" % v, [P, J, L], BF16) for v in range(2)]
+        tgt = [sbuf("tgt%d" % v, [P, J, Q], BF16) for v in range(2)]
+        gain_q = sbuf("gain_q", [P, 2, J], BF16)
+        tau_b = sbuf("tau_b", [P, Q], BF16)
+
+        x_wide = [sbuf("x_wide%d" % r, [P, D], BF16) for r in range(ROW_TILES)]
+        x_val = [sbuf("x_val%d" % i, [P, 2, 2, P, J], BF16) for i in range(4)]
+        x_cod = [sbuf("x_cod%d" % i, [P, 2, 2, P], U32) for i in range(4)]
+        x_csc = [sbuf("x_csc%d" % i, [P, 2, 2, P], U8) for i in range(4)]
+        g_val = [sbuf("g_val%d" % v, [P, J, P, J], BF16) for v in range(2)]
+        g_cod = [sbuf("g_cod%d" % v, [P, J, P], U32) for v in range(2)]
+        g_csc = [sbuf("g_csc%d" % v, [P, J, P], U8) for v in range(2)]
+        e_val = [sbuf("e_val%d" % v, [P, Q, J], BF16) for v in range(2)]
+        e_cod = [sbuf("e_cod%d" % v, [P, Q], U32) for v in range(2)]
+        e_csc = [sbuf("e_csc%d" % v, [P, Q], U8) for v in range(2)]
+        chunks = [(b, v) for b in range(2) for v in range(2)]
+        h = {k: sbuf("h%d%d" % k, [P, J, NODE_HALF], F32) for k in chunks}
+        hs_val = {k: sbuf("hs_val%d%d" % k, [P, NODE_HALF, J], BF16) for k in chunks}
+        hs_cod = {k: sbuf("hs_cod%d%d" % k, [P, NODE_HALF], U32) for k in chunks}
+        hs_csc = {k: sbuf("hs_csc%d%d" % k, [P, NODE_HALF], U8) for k in chunks}
+        hh_part = [sbuf("hh_part%d" % b, [P, 4, 2], F32) for b in range(2)]
+        hh_sum = [sbuf("hh_sum%d" % b, [P, 4], F32) for b in range(2)]
+        hh_inv = [sbuf("hh_inv%d" % b, [P, 4], F32) for b in range(2)]
+        squares = sbuf("squares", [P, BANK], BF16)
+        c_sq = [sbuf("c_sq%d" % i, [P, Q], F32) for i in range(8)]
+        res = [sbuf("res%d" % i, [P, Q], F32) for i in range(8)]
+
+        ident = sbuf("ident", [P, P], F32)
+        zeros = sbuf("zeros", [P, BANK], BF16)
+        dummy = sbuf("dummy", [P, 2], F32)
 
         banks = {}
 
-        def bank(tag, key, bufs):
-            banks[key] = psum.tile([P, 512], F32, name="ps_" + tag, tag=tag, bufs=bufs)
+        def new_bank(key, tag, bufs):
+            banks[key] = psum.tile([P, BANK], F32, name="bank_" + tag, tag=tag, bufs=bufs)
             return banks[key]
 
-        def cast_s(r, gk):
-            h, i = xrow[r]
-            sl = slice(gk * 512, (gk + 1) * 512)
-            nc.scalar.copy(xb[r][:, sl], xs[h][:, i, sl].bitcast(FP8))
+        x_place = [(i, n) for i, count in enumerate(X_LOADS) for n in range(count)]
 
-        def cast_v(r, gk):
-            h, i = xrow[r]
-            sl = slice(gk * 512, (gk + 1) * 512)
-            nc.vector.tensor_copy(out=xb[r][:, sl], in_=xs[h][:, i, sl].bitcast(FP8))
+        def x_widen(copy, r, k0, k1):
+            i, n = x_place[r]
+            copy(x_wide[r][:, k0:k1], x_raw[i][:, n, k0:k1].bitcast(FP8))
 
-        def x_t(r, gk):
-            if gk == 0:
-                bank("tr", ("x", r), TR)
-            b = banks["x", r]
-            words = xb[r][:].bitcast(F32)
-            for u in range(2):
-                i = 2 * gk + u
-                nc.tensor.transpose(b[:, i * P : (i + 1) * P], words[:, 256 * gk + u : 256 * (gk + 1) : 2], ident[:])
+        def x_turn(r):
+            bank = new_bank(("x", r), "turned", TURNED_BANKS)
+            words = x_wide[r][:].bitcast(F32)
+            for v in range(2):
+                for u in range(2):
+                    at = (2 * v + u) * P
+                    nc.tensor.transpose(
+                        bank[:, at : at + P], words[:, 256 * v + u : 256 * (v + 1) : 2], ident[:]
+                    )
 
-        def x_e(r, gk):
-            b = banks["x", r]
-            src = b[:, gk * 256 : (gk + 1) * 256].bitcast(BF16).rearrange("p (u r e) -> p r u e", u=2, e=2)
-            sc = xsc[:, gk, :].rearrange("p (u e) -> p u e", u=2).unsqueeze(1).to_broadcast([P, P, 2, 2])
-            dst = xg[r][:, gk].rearrange("p r (u e) -> p r u e", u=2)
-            nc.vector.tensor_tensor(out=dst, in0=src, in1=sc, op=ALU.mult)
-
-        def x_q(r):
-            nc.vector.quantize_mx(
-                out=xcod[r][:].rearrange("p g r -> p (g r)").bitcast(FP8X4),
-                scales=xcsc[r][:].rearrange("p g r -> p (g r)"),
-                in_=xg[r][:].rearrange("p g r k -> p (g r k)"),
+        def x_scale_out(r, v):
+            turned = banks["x", r][:, 256 * v : 256 * (v + 1)].bitcast(BF16)
+            nc.vector.tensor_tensor(
+                out=x_val[r // 2][:, r % 2, v].rearrange("p r (u e) -> p r u e", u=2),
+                in0=turned.rearrange("p (u r e) -> p r u e", u=2, e=2),
+                in1=x_scl[:, v, :].rearrange("p (u e) -> p u e", u=2).unsqueeze(1).to_broadcast([P, P, 2, 2]),
+                op=ALU.mult,
             )
 
-        def mm(r, f):
-            b = bank("mm", ("m", r, f), MM)
-            for gk in range(2):
+        def x_quantise(r):
+            i, n = r // 2, r % 2
+            nc.vector.quantize_mx(
+                out=x_cod[i][:, n].rearrange("p v r -> p (v r)").bitcast(FP8X4),
+                scales=x_csc[i][:, n].rearrange("p v r -> p (v r)"),
+                in_=x_val[i][:, n].rearrange("p v r j -> p (v r j)"),
+            )
+
+        def x_quantise_pair(i):
+            nc.vector.quantize_mx(
+                out=x_cod[i][:].rearrange("p n v r -> p (n v r)").bitcast(FP8X4),
+                scales=x_csc[i][:].rearrange("p n v r -> p (n v r)"),
+                in_=x_val[i][:].rearrange("p n v r j -> p (n v r j)"),
+            )
+
+        def preact(r, b):
+            bank = new_bank(("xw", r, b), "preact", PREACT_BANKS)
+            for v in range(2):
                 nc.tensor.matmul_mx(
-                    out=b[:],
-                    lhsT=xcod[r][:, gk, :].bitcast(FP8X4),
-                    lhsT_scale=xcsc[r][:, gk, :],
-                    rhs=wwd[f][:, gk, :].bitcast(FP4X4),
-                    rhs_scale=wsc[:, gk, f * 512 : (f + 1) * 512],
-                    start=(gk == 0),
-                    stop=(gk == 1),
+                    out=bank[:],
+                    lhsT=x_cod[r // 2][:, r % 2, v, :].bitcast(FP8X4),
+                    lhsT_scale=x_csc[r // 2][:, r % 2, v, :],
+                    rhs=w_wrd[b][:, v, :].bitcast(FP4X4),
+                    rhs_scale=w_scl[:, v, b * NODE_HALF : (b + 1) * NODE_HALF],
+                    start=(v == 0),
+                    stop=(v == 1),
                 )
 
-        def tanh(r, f):
-            nc.scalar.activation(out=hh[f, r // 4][:, r % 4, :], in_=banks["m", r, f][:], func=ACT.Tanh)
+        def tanh(r, b):
+            nc.scalar.activation(out=h[b, r // J][:, r % J, :], in_=banks["xw", r, b][:], func=ACT.Tanh)
 
-        def g_t(j):
-            b = bank("tr", ("g", j), TR)
-            for i in range(2):
-                words = gs[j // 2][:, 2 * (j % 2) + i, :].bitcast(F32)
+        def g_turn(i):
+            bank = new_bank(("g", i), "turned", TURNED_BANKS)
+            for n in range(2):
+                words = hid[i // 2][:, 2 * (i % 2) + n, :].bitcast(F32)
                 for u in range(2):
-                    k = 2 * i + u
-                    nc.tensor.transpose(b[:, k * P : (k + 1) * P], words[:, u:256:2], ident[:])
+                    at = (2 * n + u) * P
+                    nc.tensor.transpose(bank[:, at : at + P], words[:, u:256:2], ident[:])
 
-        def g_e(j):
+        def g_copy_out(i):
+            n = 2 * (i % 2)
             nc.scalar.copy(
-                gg[j][:].bitcast(F32),
-                banks["g", j][:].rearrange("p (i u r) -> p i r u", i=2, u=2),
+                g_val[i // 2][:, n : n + 2].bitcast(F32),
+                banks["g", i][:].rearrange("p (n u r) -> p n r u", n=2, u=2),
             )
 
-        def g_q(j):
+        def g_quantise(v):
             nc.vector.quantize_mx(
-                out=gcod[j][:].rearrange("p i r -> p (i r)").bitcast(FP8X4),
-                scales=gcsc[j][:].rearrange("p i r -> p (i r)"),
-                in_=gg[j][:].rearrange("p i r k -> p (i r k)"),
+                out=g_cod[v][:].rearrange("p n r -> p (n r)").bitcast(FP8X4),
+                scales=g_csc[v][:].rearrange("p n r -> p (n r)"),
+                in_=g_val[v][:].rearrange("p n r j -> p (n r j)"),
             )
 
-        def beta(gi, qb):
-            b = bank("ec", ("b", gi, qb), EC)
-            for tt in range(4):
-                j, i = 2 * gi + tt // 2, tt % 2
+        def beta_product(v, qb):
+            bank = new_bank(("gb", v, qb), "product", PRODUCT_BANKS)
+            for j in range(J):
                 nc.tensor.matmul_mx(
-                    out=b[:, tt * P : (tt + 1) * P],
-                    lhsT=gcod[j][:, i, :].bitcast(FP8X4),
-                    lhsT_scale=gcsc[j][:, i, :],
-                    rhs=bwd[:, qb * 256 : (qb + 1) * 256].bitcast(FP4X4),
-                    rhs_scale=bsc[:, qb * P : (qb + 1) * P],
+                    out=bank[:, j * P : (j + 1) * P],
+                    lhsT=g_cod[v][:, j, :].bitcast(FP8X4),
+                    lhsT_scale=g_csc[v][:, j, :],
+                    rhs=b_wrd[:, qb * P * FP4_BYTES : (qb + 1) * P * FP4_BYTES].bitcast(FP4X4),
+                    rhs_scale=b_scl[:, qb * P : (qb + 1) * P],
                     start=True,
                     stop=True,
                 )
 
-        def e_s(gi, qb):
+        def residual(v, qb):
+            cols = slice(qb * P, (qb + 1) * P)
             nc.vector.tensor_tensor(
-                out=eb[gi][:, qb * P : (qb + 1) * P, :].rearrange("p (c i) t -> p c t i", i=4),
-                in0=ts[gi][:, :, qb * P : (qb + 1) * P].rearrange("p t (c i) -> p c t i", i=4),
-                in1=banks["b", gi, qb][:].rearrange("p (t c i) -> p c t i", t=4, i=4),
+                out=e_val[v][:, cols, :].rearrange("p (c i) j -> p c j i", i=4),
+                in0=tgt[v][:, :, cols].rearrange("p j (c i) -> p c j i", i=4),
+                in1=banks["gb", v, qb][:].rearrange("p (j c i) -> p c j i", j=J, i=4),
                 op=ALU.subtract,
             )
 
-        def e_q(gi):
+        def e_quantise(v):
             nc.vector.quantize_mx(
-                out=ecod[gi][:].bitcast(FP8X4), scales=ecsc[gi][:], in_=eb[gi][:].rearrange("p q t -> p (q t)")
+                out=e_cod[v][:].bitcast(FP8X4), scales=e_csc[v][:], in_=e_val[v][:].rearrange("p q j -> p (q j)")
             )
 
-        def h_t(f, gi, fb):
-            b = bank("tr", ("h", f, gi, fb), TR)
-            for tt in range(4):
-                nc.tensor.transpose(b[:, tt * P : (tt + 1) * P], hh[f, gi][:, tt, fb * P : (fb + 1) * P], ident[:])
+        def h_turn(b, v, nb):
+            bank = new_bank(("h", b, v, nb), "turned", TURNED_BANKS)
+            for j in range(J):
+                nc.tensor.transpose(bank[:, j * P : (j + 1) * P], h[b, v][:, j, nb * P : (nb + 1) * P], ident[:])
 
-        def sq(f, gi, fb):
+        def energy(b, v, nb):
             nc.scalar.activation(
-                out=junk[:], in_=banks["h", f, gi, fb][:], func=ACT.Square, accum_out=part[f][:, fb, gi : gi + 1]
+                out=squares[:],
+                in_=banks["h", b, v, nb][:],
+                func=ACT.Square,
+                accum_out=hh_part[b][:, nb, v : v + 1],
             )
 
-        def hs(eng, f, gi, qu):
-            sl = slice(qu * P, (qu + 1) * P)
-            eng.tensor_tensor(
-                out=hsb[f, gi][:, sl, :].rearrange("p (c i) t -> p c t i", i=4),
-                in0=hh[f, gi][:, :, sl].rearrange("p t (c i) -> p c t i", i=4),
-                in1=s4[:, gi, :].unsqueeze(1).unsqueeze(3).to_broadcast([P, 32, 4, 4]),
+        def energy_inverse(b):
+            nc.vector.tensor_tensor(out=hh_sum[b][:], in0=hh_part[b][:, :, 0], in1=hh_part[b][:, :, 1], op=ALU.add)
+            nc.vector.reciprocal(out=hh_inv[b][:], in_=hh_sum[b][:])
+
+        def apply_gain(b, v, part):
+            cols = slice(part * 256, (part + 1) * 256)
+            nc.vector.tensor_tensor(
+                out=hs_val[b, v][:, cols, :].rearrange("p (c i) j -> p c j i", i=4),
+                in0=h[b, v][:, :, cols].rearrange("p j (c i) -> p c j i", i=4),
+                in1=gain_q[:, v, :].unsqueeze(1).unsqueeze(3).to_broadcast([P, 64, J, 4]),
                 op=ALU.mult,
             )
 
-        def h_v(f, gi, qu):
-            hs(nc.vector, f, gi, qu)
-
-        def h_g(f, gi, qu):
-            hs(nc.gpsimd, f, gi, qu)
-
-        def h_q(f, gi, half):
-            sl = slice(half * 256, (half + 1) * 256)
+        def hs_quantise(b, v, n0, n1):
             nc.vector.quantize_mx(
-                out=hcod[f, gi][:, sl].bitcast(FP8X4),
-                scales=hcsc[f, gi][:, sl],
-                in_=hsb[f, gi][:, sl, :].rearrange("p f t -> p (f t)"),
+                out=hs_cod[b, v][:, n0:n1].bitcast(FP8X4),
+                scales=hs_csc[b, v][:, n0:n1],
+                in_=hs_val[b, v][:, n0:n1, :].rearrange("p f j -> p (f j)"),
             )
 
-        def rec(f):
-            nc.vector.tensor_tensor(out=hsum[f][:], in0=part[f][:, :, 0], in1=part[f][:, :, 1], op=ALU.add)
-            nc.vector.reciprocal(out=rinv[f][:], in_=hsum[f][:])
+        def correlate(b, nb):
+            bank = new_bank(("c", b, nb), "product", PRODUCT_BANKS)
+            cols = slice(nb * P, (nb + 1) * P)
+            for v in range(2):
+                nc.tensor.matmul_mx(
+                    out=bank[:],
+                    lhsT=hs_cod[b, v][:, cols].bitcast(FP8X4),
+                    lhsT_scale=hs_csc[b, v][:, cols],
+                    rhs=e_cod[v][:].bitcast(FP8X4),
+                    rhs_scale=e_csc[v][:],
+                    start=(v == 0),
+                    stop=(v == 1),
+                )
 
-        def c_mm(gi, f, fb):
-            if gi == 0:
-                bank("ec", ("c", f, fb), EC)
-            nc.tensor.matmul_mx(
-                out=banks["c", f, fb][:],
-                lhsT=hcod[f, gi][:, fb * P : (fb + 1) * P].bitcast(FP8X4),
-                lhsT_scale=hcsc[f, gi][:, fb * P : (fb + 1) * P],
-                rhs=ecod[gi][:].bitcast(FP8X4),
-                rhs_scale=ecsc[gi][:],
-                start=(gi == 0),
-                stop=(gi == 1),
-            )
+        def square(b, nb):
+            nc.scalar.activation(out=c_sq[4 * b + nb][:], in_=banks["c", b, nb][:], func=ACT.Square)
 
-        def c0(f, fb):
-            c_mm(0, f, fb)
+        def score(b, nb, parts=1):
+            i = 4 * b + nb
+            width = Q // parts
+            for n in range(parts):
+                cols = slice(n * width, (n + 1) * width)
+                nc.vector.scalar_tensor_tensor(
+                    out=res[i][:, cols],
+                    in0=c_sq[i][:, cols],
+                    scalar=hh_inv[b][:, nb : nb + 1],
+                    in1=tau_b[:, cols],
+                    op0=ALU.mult,
+                    op1=ALU.subtract,
+                )
+                nc.sync.dma_start(out=out[i * P : (i + 1) * P, cols], in_=res[i][:, cols])
 
-        def c1(f, fb):
-            c_mm(1, f, fb)
-
-        def c_sq(f, fb):
-            nc.scalar.activation(out=csqs[4 * f + fb][:], in_=banks["c", f, fb][:], func=ACT.Square)
-
-        def o(f, fb):
-            k = 4 * f + fb
-            nc.vector.scalar_tensor_tensor(
-                out=outs[k][:], in0=csqs[k][:], scalar=rinv[f][:, fb : fb + 1], in1=taub[:], op0=ALU.mult, op1=ALU.subtract
-            )
-            nc.sync.dma_start(out=out[k * P : (k + 1) * P, :], in_=outs[k][:])
-
-        STEP = {
-            "castS": cast_s, "castV": cast_v, "xT": x_t, "xE": x_e, "xQ": x_q, "mm": mm, "tanh": tanh,
-            "gT": g_t, "gE": g_e, "gQ": g_q, "beta": beta, "es": e_s, "eQ": e_q, "hT": h_t, "sq": sq,
-            "hq": h_v, "hG": h_g, "hQ": h_q, "rec": rec, "c0": c0, "c1": c1, "csq": c_sq, "out": o,
-        }
-
-        wz = kt("wz", [P, 512], BF16)
-        nc.vector.memset(wz[:], 0.0)
-        wb = bank("ec", "warm", EC)
-        for i in range(5):
-            nc.tensor.matmul(wb[:], wz[:, 0:P], wz[:], start=True, stop=True)
         make_identity(nc, ident[:])
-        nc.vector.memset(warm[:], 0.0)
-        nc.scalar.activation(out=warm[:, 1:2], in_=warm[:, 0:1], func=ACT.Tanh)
-        nc.vector.memset(wsc[:].rearrange("p g n -> p (g n)").bitcast(I32), 0)
-        nc.vector.memset(bsc[:].bitcast(I32), 0)
+        nc.vector.memset(dummy[:], 0.0)
+        nc.scalar.activation(out=dummy[:, 1:2], in_=dummy[:, 0:1], func=ACT.Tanh)
+        nc.vector.memset(w_scl[:].rearrange("p v n -> p (v n)").bitcast(I32), 0)
+        nc.vector.memset(b_scl[:].bitcast(I32), 0)
+        nc.vector.memset(zeros[:], 0.0)
+        warm = new_bank("warm", "product", PRODUCT_BANKS)
+        for n in range(WARM_UP_MATMULS):
+            nc.tensor.matmul(warm[:], zeros[:, 0:P], zeros[:], start=True, stop=True)
 
-        xv = x_bytes.rearrange("(g p t) k -> g p t k", p=P, t=4)
-        ld = nc.sync.dma_start
+        load = nc.sync.dma_start
+        x_rows = x_bytes.rearrange("(v p j) k -> v p j k", p=P, j=J)
+        hid_rows = hidden.rearrange("(v p j) k -> v p j k", p=P, j=J)
+        tgt_rows = target.rearrange("(v p j) q -> v p j q", p=P, j=J)
+        w_rows = w_words.rearrange("v p n -> p v n")
 
-        def ldx(h):
-            r0 = sum(X_LOADS[:h])
-            ld(out=xs[h][:], in_=xv[r0 // 4][:, r0 % 4 : r0 % 4 + X_LOADS[h], :])
+        def load_x(i):
+            r = sum(X_LOADS[:i])
+            load(out=x_raw[i][:], in_=x_rows[r // J][:, r % J : r % J + X_LOADS[i], :])
 
-        wv = w_words.rearrange("g p n -> p g n")
-        gv = g.rearrange("(g p t) k -> g p t k", p=P, t=4)
-        tv = t.rearrange("(g p t) k -> g p t k", p=P, t=4)
-        ldx(0)
-        ldx(1)
-        ld(out=xsc[:], in_=x_scale.rearrange("o (g p t) -> p (o g) t", p=P, t=4))
-        ldx(2)
-        ld(out=wwd[0][:].bitcast(I32), in_=wv[:, :, 0:1024].bitcast(I32))
-        for qd in range(4):
-            ld(
-                out=wsc[32 * qd : 32 * qd + 4, :, :].bitcast(I32),
-                in_=w_scales[:, 4 * qd : 4 * qd + 4, :].rearrange("g r n -> r g n").bitcast(I32),
+        def load_w(b):
+            width = FP4_BYTES * NODE_HALF
+            load(out=w_wrd[b][:].bitcast(I32), in_=w_rows[:, :, b * width : (b + 1) * width].bitcast(I32))
+
+        load_x(0)
+        load_x(1)
+        load(out=x_scl[:], in_=x_scale.rearrange("o (v p j) -> p (o v) j", p=P, j=J))
+        load_x(2)
+        load_w(0)
+        for quadrant in range(4):
+            load(
+                out=w_scl[32 * quadrant : 32 * quadrant + 4, :, :].bitcast(I32),
+                in_=w_scales[:, 4 * quadrant : 4 * quadrant + 4, :].rearrange("v r n -> r v n").bitcast(I32),
             )
-        ldx(3)
-        ld(out=s4[:], in_=s.rearrange("(g p t) -> p g t", p=P, t=4))
-        ld(out=gs[0][:], in_=gv[0])
-        ld(out=wwd[1][:].bitcast(I32), in_=wv[:, :, 1024:2048].bitcast(I32))
-        ld(out=bwd[:].bitcast(I32), in_=beta_words[0].bitcast(I32))
-        for qd in range(4):
-            ld(
-                out=bsc[32 * qd : 32 * qd + 4, :].bitcast(I32),
-                in_=beta_scales[0][4 * qd : 4 * qd + 4, :].bitcast(I32),
+        load_x(3)
+        load(out=gain_q[:], in_=gain.rearrange("(v p j) -> p v j", p=P, j=J))
+        load(out=hid[0][:], in_=hid_rows[0])
+        load_w(1)
+        load(out=b_wrd[:].bitcast(I32), in_=beta_words[0].bitcast(I32))
+        for quadrant in range(4):
+            load(
+                out=b_scl[32 * quadrant : 32 * quadrant + 4, :].bitcast(I32),
+                in_=beta_scales[0][4 * quadrant : 4 * quadrant + 4, :].bitcast(I32),
             )
-        ld(out=gs[1][:], in_=gv[1])
-        ld(out=ts[0][:], in_=tv[0])
-        ld(out=ts[1][:], in_=tv[1])
-        ld(out=taub[:], in_=tau.partition_broadcast(P))
+        load(out=hid[1][:], in_=hid_rows[1])
+        load(out=tgt[0][:], in_=tgt_rows[0])
+        load(out=tgt[1][:], in_=tgt_rows[1])
+        load(out=tau_b[:], in_=tau.partition_broadcast(P))
 
         with tc.manual_schedule():
-            for st in ORDER:
-                STEP[st[0]](*st[1:])
+            for r in range(-3, ROW_TILES + 2):
+                if r + 3 == 0:
+                    x_widen(nc.vector.tensor_copy, 0, 0, 512)
+                    x_widen(nc.scalar.copy, 0, 512, D)
+                elif r + 3 == 1:
+                    x_widen(nc.vector.tensor_copy, 1, 0, D)
+                elif r + 3 < ROW_TILES:
+                    x_widen(nc.scalar.copy, r + 3, 0, D)
+                if 0 <= r + 1 < ROW_TILES:
+                    x_turn(r + 1)
+                if 0 <= r - 5 < 4:
+                    g_turn(r - 5)
+                    g_copy_out(r - 5)
+                if 0 <= r < ROW_TILES:
+                    x_scale_out(r, 0)
+                if 0 <= r - 1 < SINGLE_ROW_TILES:
+                    x_quantise(r - 1)
+                elif SINGLE_ROW_TILES < r <= ROW_TILES and r % 2 == 0:
+                    x_quantise_pair(r // 2 - 1)
+                if 0 <= r < ROW_TILES:
+                    x_scale_out(r, 1)
+                if 0 <= r - 2:
+                    preact(r - 2, 0)
+                    tanh(r - 2, 0)
+                if 0 <= r - 5 < 2:
+                    preact(r - 5, 1)
+                    tanh(r - 5, 1)
+                if r == 7:
+                    apply_gain(0, 0, 0)
+                if r == 8:
+                    g_quantise(0)
+
+            beta_product(0, 0)
+            beta_product(0, 1)
+            for step in range(0, 8, 2):
+                pair = (divmod(step, 4), divmod(step + 1, 4))
+                ahead = (step + 2, step + 3) if step < 6 else ()
+                for k in ahead:
+                    preact(k, 1)
+                for k in ahead:
+                    beta_product(*divmod(k, 4))
+                for k in ahead:
+                    tanh(k, 1)
+                for v, nb in pair:
+                    h_turn(0, v, nb)
+                if step < 6:
+                    apply_gain(0, *divmod(step // 2 + 1, 2))
+                if step == 0:
+                    g_quantise(1)
+                for v, qb in pair:
+                    residual(v, qb)
+                for v, nb in pair:
+                    energy(0, v, nb)
+                if step == 4:
+                    e_quantise(0)
+                else:
+                    if step > 0:
+                        hs_quantise(0, step // 4, 0, NODE_HALF)
+            e_quantise(1)
+
+            for step in range(0, 8, 2):
+                pair = (divmod(step, 4), divmod(step + 1, 4))
+                for v, nb in pair:
+                    h_turn(1, v, nb)
+                blocks = (step - 2, step - 1) if step in (2, 4) else ()
+                for nb in blocks:
+                    correlate(0, nb)
+                for v, nb in pair:
+                    energy(1, v, nb)
+                for nb in blocks:
+                    square(0, nb)
+            apply_gain(1, 0, 0)
+            apply_gain(1, 0, 1)
+            energy_inverse(0)
+            apply_gain(1, 1, 0)
+            hs_quantise(1, 0, 0, NODE_HALF)
+            apply_gain(1, 1, 1)
+            hs_quantise(1, 1, 0, 256)
+            hs_quantise(1, 1, 256, NODE_HALF)
+
+            for nb in (0, 1):
+                correlate(1, nb)
+                square(1, nb)
+            for nb in (0, 1, 2):
+                score(0, nb)
+            energy_inverse(1)
+            score(0, 3)
+            for nb in range(4):
+                if nb + 2 < 4:
+                    correlate(1, nb + 2)
+                    square(1, nb + 2)
+                score(1, nb, parts=LAST_BLOCK_PARTS if nb == 3 else 1)

from contextlib import ExitStack

import concourse.mybir as mybir
from concourse.masks import make_identity

F32 = mybir.dt.float32
BF16 = mybir.dt.bfloat16
I32 = mybir.dt.int32
U32 = mybir.dt.uint32
U8 = mybir.dt.uint8
FP8 = mybir.dt.float8_e4m3fn
FP8X4 = mybir.dt.float8_e4m3fn_x4
FP4X4 = mybir.dt.float4_e2m1fn_x4
ACT = mybir.ActivationFunctionType
ALU = mybir.AluOpType

N, D, F, L, Q = 1024, 1024, 1024, 512, 512
FLOPS = 2 * N * D * F + 2 * N * L * Q + 2 * N * F * Q

P = 128
J = 4
BANK = 512
ROW_TILES = N // P
NODE_HALF = F // 2
FP4_BYTES = 2

X_LOADS = (1, 1, 2, 4)
SINGLE_ROW_TILES = 4
WARM_UP_MATMULS = 5
LAST_BLOCK_PARTS = 2

TURNED_BANKS = 4
PREACT_BANKS = 2
PRODUCT_BANKS = 2


def tile_stochasticconfigurationcandidatescores_w4_kernel(
    tc, x_bytes, x_scale, w_words, w_scales, gain, target, hidden, beta_words, beta_scales, tau, out
):
    nc = tc.nc
    with ExitStack() as ctx:
        keep = ctx.enter_context(tc.tile_pool(name="keep", bufs=1))
        psum = ctx.enter_context(tc.psum_pool(name="psum", bufs=1))

        def sbuf(name, shape, dtype):
            return keep.tile(shape, dtype, name=name, align_bytes=64)

        x_raw = [sbuf("x_raw%d" % i, [P, n, D], U8) for i, n in enumerate(X_LOADS)]
        x_scl = sbuf("x_scl", [P, 2, J], F32)
        w_wrd = [sbuf("w_wrd%d" % b, [P, 2, FP4_BYTES * NODE_HALF], U8) for b in range(2)]
        w_scl = sbuf("w_scl", [P, 2, F], U8)
        b_wrd = sbuf("b_wrd", [P, FP4_BYTES * Q], U8)
        b_scl = sbuf("b_scl", [P, Q], U8)
        hid = [sbuf("hid%d" % v, [P, J, L], BF16) for v in range(2)]
        tgt = [sbuf("tgt%d" % v, [P, J, Q], BF16) for v in range(2)]
        gain_q = sbuf("gain_q", [P, 2, J], BF16)
        tau_b = sbuf("tau_b", [P, Q], BF16)

        x_wide = [sbuf("x_wide%d" % r, [P, D], BF16) for r in range(ROW_TILES)]
        x_val = [sbuf("x_val%d" % i, [P, 2, 2, P, J], BF16) for i in range(4)]
        x_cod = [sbuf("x_cod%d" % i, [P, 2, 2, P], U32) for i in range(4)]
        x_csc = [sbuf("x_csc%d" % i, [P, 2, 2, P], U8) for i in range(4)]
        g_val = [sbuf("g_val%d" % v, [P, J, P, J], BF16) for v in range(2)]
        g_cod = [sbuf("g_cod%d" % v, [P, J, P], U32) for v in range(2)]
        g_csc = [sbuf("g_csc%d" % v, [P, J, P], U8) for v in range(2)]
        e_val = [sbuf("e_val%d" % v, [P, Q, J], BF16) for v in range(2)]
        e_cod = [sbuf("e_cod%d" % v, [P, Q], U32) for v in range(2)]
        e_csc = [sbuf("e_csc%d" % v, [P, Q], U8) for v in range(2)]
        chunks = [(b, v) for b in range(2) for v in range(2)]
        h = {k: sbuf("h%d%d" % k, [P, J, NODE_HALF], F32) for k in chunks}
        hs_val = {k: sbuf("hs_val%d%d" % k, [P, NODE_HALF, J], BF16) for k in chunks}
        hs_cod = {k: sbuf("hs_cod%d%d" % k, [P, NODE_HALF], U32) for k in chunks}
        hs_csc = {k: sbuf("hs_csc%d%d" % k, [P, NODE_HALF], U8) for k in chunks}
        hh_part = [sbuf("hh_part%d" % b, [P, 4, 2], F32) for b in range(2)]
        hh_sum = [sbuf("hh_sum%d" % b, [P, 4], F32) for b in range(2)]
        hh_inv = [sbuf("hh_inv%d" % b, [P, 4], F32) for b in range(2)]
        squares = sbuf("squares", [P, BANK], BF16)
        c_sq = [sbuf("c_sq%d" % i, [P, Q], F32) for i in range(8)]
        res = [sbuf("res%d" % i, [P, Q], F32) for i in range(8)]

        ident = sbuf("ident", [P, P], F32)
        zeros = sbuf("zeros", [P, BANK], BF16)
        dummy = sbuf("dummy", [P, 2], F32)

        banks = {}

        def new_bank(key, tag, bufs):
            banks[key] = psum.tile([P, BANK], F32, name="bank_" + tag, tag=tag, bufs=bufs)
            return banks[key]

        x_place = [(i, n) for i, count in enumerate(X_LOADS) for n in range(count)]

        def x_widen(copy, r, k0, k1):
            i, n = x_place[r]
            copy(x_wide[r][:, k0:k1], x_raw[i][:, n, k0:k1].bitcast(FP8))

        def x_turn(r):
            bank = new_bank(("x", r), "turned", TURNED_BANKS)
            words = x_wide[r][:].bitcast(F32)
            for v in range(2):
                for u in range(2):
                    at = (2 * v + u) * P
                    nc.tensor.transpose(
                        bank[:, at : at + P], words[:, 256 * v + u : 256 * (v + 1) : 2], ident[:]
                    )

        def x_scale_out(r, v):
            turned = banks["x", r][:, 256 * v : 256 * (v + 1)].bitcast(BF16)
            nc.vector.tensor_tensor(
                out=x_val[r // 2][:, r % 2, v].rearrange("p r (u e) -> p r u e", u=2),
                in0=turned.rearrange("p (u r e) -> p r u e", u=2, e=2),
                in1=x_scl[:, v, :].rearrange("p (u e) -> p u e", u=2).unsqueeze(1).to_broadcast([P, P, 2, 2]),
                op=ALU.mult,
            )

        def x_quantise(r):
            i, n = r // 2, r % 2
            nc.vector.quantize_mx(
                out=x_cod[i][:, n].rearrange("p v r -> p (v r)").bitcast(FP8X4),
                scales=x_csc[i][:, n].rearrange("p v r -> p (v r)"),
                in_=x_val[i][:, n].rearrange("p v r j -> p (v r j)"),
            )

        def x_quantise_pair(i):
            nc.vector.quantize_mx(
                out=x_cod[i][:].rearrange("p n v r -> p (n v r)").bitcast(FP8X4),
                scales=x_csc[i][:].rearrange("p n v r -> p (n v r)"),
                in_=x_val[i][:].rearrange("p n v r j -> p (n v r j)"),
            )

        def preact(r, b):
            bank = new_bank(("xw", r, b), "preact", PREACT_BANKS)
            for v in range(2):
                nc.tensor.matmul_mx(
                    out=bank[:],
                    lhsT=x_cod[r // 2][:, r % 2, v, :].bitcast(FP8X4),
                    lhsT_scale=x_csc[r // 2][:, r % 2, v, :],
                    rhs=w_wrd[b][:, v, :].bitcast(FP4X4),
                    rhs_scale=w_scl[:, v, b * NODE_HALF : (b + 1) * NODE_HALF],
                    start=(v == 0),
                    stop=(v == 1),
                )

        def tanh(r, b):
            nc.scalar.activation(out=h[b, r // J][:, r % J, :], in_=banks["xw", r, b][:], func=ACT.Tanh)

        def g_turn(i):
            bank = new_bank(("g", i), "turned", TURNED_BANKS)
            for n in range(2):
                words = hid[i // 2][:, 2 * (i % 2) + n, :].bitcast(F32)
                for u in range(2):
                    at = (2 * n + u) * P
                    nc.tensor.transpose(bank[:, at : at + P], words[:, u:256:2], ident[:])

        def g_copy_out(i):
            n = 2 * (i % 2)
            nc.scalar.copy(
                g_val[i // 2][:, n : n + 2].bitcast(F32),
                banks["g", i][:].rearrange("p (n u r) -> p n r u", n=2, u=2),
            )

        def g_quantise(v):
            nc.vector.quantize_mx(
                out=g_cod[v][:].rearrange("p n r -> p (n r)").bitcast(FP8X4),
                scales=g_csc[v][:].rearrange("p n r -> p (n r)"),
                in_=g_val[v][:].rearrange("p n r j -> p (n r j)"),
            )

        def beta_product(v, qb):
            bank = new_bank(("gb", v, qb), "product", PRODUCT_BANKS)
            for j in range(J):
                nc.tensor.matmul_mx(
                    out=bank[:, j * P : (j + 1) * P],
                    lhsT=g_cod[v][:, j, :].bitcast(FP8X4),
                    lhsT_scale=g_csc[v][:, j, :],
                    rhs=b_wrd[:, qb * P * FP4_BYTES : (qb + 1) * P * FP4_BYTES].bitcast(FP4X4),
                    rhs_scale=b_scl[:, qb * P : (qb + 1) * P],
                    start=True,
                    stop=True,
                )

        def residual(v, qb):
            cols = slice(qb * P, (qb + 1) * P)
            nc.vector.tensor_tensor(
                out=e_val[v][:, cols, :].rearrange("p (c i) j -> p c j i", i=4),
                in0=tgt[v][:, :, cols].rearrange("p j (c i) -> p c j i", i=4),
                in1=banks["gb", v, qb][:].rearrange("p (j c i) -> p c j i", j=J, i=4),
                op=ALU.subtract,
            )

        def e_quantise(v):
            nc.vector.quantize_mx(
                out=e_cod[v][:].bitcast(FP8X4), scales=e_csc[v][:], in_=e_val[v][:].rearrange("p q j -> p (q j)")
            )

        def h_turn(b, v, nb):
            bank = new_bank(("h", b, v, nb), "turned", TURNED_BANKS)
            for j in range(J):
                nc.tensor.transpose(bank[:, j * P : (j + 1) * P], h[b, v][:, j, nb * P : (nb + 1) * P], ident[:])

        def energy(b, v, nb):
            nc.scalar.activation(
                out=squares[:],
                in_=banks["h", b, v, nb][:],
                func=ACT.Square,
                accum_out=hh_part[b][:, nb, v : v + 1],
            )

        def energy_inverse(b):
            nc.vector.tensor_tensor(out=hh_sum[b][:], in0=hh_part[b][:, :, 0], in1=hh_part[b][:, :, 1], op=ALU.add)
            nc.vector.reciprocal(out=hh_inv[b][:], in_=hh_sum[b][:])

        def apply_gain(b, v, part):
            cols = slice(part * 256, (part + 1) * 256)
            nc.vector.tensor_tensor(
                out=hs_val[b, v][:, cols, :].rearrange("p (c i) j -> p c j i", i=4),
                in0=h[b, v][:, :, cols].rearrange("p j (c i) -> p c j i", i=4),
                in1=gain_q[:, v, :].unsqueeze(1).unsqueeze(3).to_broadcast([P, 64, J, 4]),
                op=ALU.mult,
            )

        def hs_quantise(b, v, n0, n1):
            nc.vector.quantize_mx(
                out=hs_cod[b, v][:, n0:n1].bitcast(FP8X4),
                scales=hs_csc[b, v][:, n0:n1],
                in_=hs_val[b, v][:, n0:n1, :].rearrange("p f j -> p (f j)"),
            )

        def correlate(b, nb):
            bank = new_bank(("c", b, nb), "product", PRODUCT_BANKS)
            cols = slice(nb * P, (nb + 1) * P)
            for v in range(2):
                nc.tensor.matmul_mx(
                    out=bank[:],
                    lhsT=hs_cod[b, v][:, cols].bitcast(FP8X4),
                    lhsT_scale=hs_csc[b, v][:, cols],
                    rhs=e_cod[v][:].bitcast(FP8X4),
                    rhs_scale=e_csc[v][:],
                    start=(v == 0),
                    stop=(v == 1),
                )

        def square(b, nb):
            nc.scalar.activation(out=c_sq[4 * b + nb][:], in_=banks["c", b, nb][:], func=ACT.Square)

        def score(b, nb, parts=1):
            i = 4 * b + nb
            width = Q // parts
            for n in range(parts):
                cols = slice(n * width, (n + 1) * width)
                nc.vector.scalar_tensor_tensor(
                    out=res[i][:, cols],
                    in0=c_sq[i][:, cols],
                    scalar=hh_inv[b][:, nb : nb + 1],
                    in1=tau_b[:, cols],
                    op0=ALU.mult,
                    op1=ALU.subtract,
                )
                nc.sync.dma_start(out=out[i * P : (i + 1) * P, cols], in_=res[i][:, cols])

        make_identity(nc, ident[:])
        nc.vector.memset(dummy[:], 0.0)
        nc.scalar.activation(out=dummy[:, 1:2], in_=dummy[:, 0:1], func=ACT.Tanh)
        nc.vector.memset(w_scl[:].rearrange("p v n -> p (v n)").bitcast(I32), 0)
        nc.vector.memset(b_scl[:].bitcast(I32), 0)
        nc.vector.memset(zeros[:], 0.0)
        warm = new_bank("warm", "product", PRODUCT_BANKS)
        for n in range(WARM_UP_MATMULS):
            nc.tensor.matmul(warm[:], zeros[:, 0:P], zeros[:], start=True, stop=True)

        load = nc.sync.dma_start
        x_rows = x_bytes.rearrange("(v p j) k -> v p j k", p=P, j=J)
        hid_rows = hidden.rearrange("(v p j) k -> v p j k", p=P, j=J)
        tgt_rows = target.rearrange("(v p j) q -> v p j q", p=P, j=J)
        w_rows = w_words.rearrange("v p n -> p v n")

        def load_x(i):
            r = sum(X_LOADS[:i])
            load(out=x_raw[i][:], in_=x_rows[r // J][:, r % J : r % J + X_LOADS[i], :])

        def load_w(b):
            width = FP4_BYTES * NODE_HALF
            load(out=w_wrd[b][:].bitcast(I32), in_=w_rows[:, :, b * width : (b + 1) * width].bitcast(I32))

        load_x(0)
        load_x(1)
        load(out=x_scl[:], in_=x_scale.rearrange("o (v p j) -> p (o v) j", p=P, j=J))
        load_x(2)
        load_w(0)
        for quadrant in range(4):
            load(
                out=w_scl[32 * quadrant : 32 * quadrant + 4, :, :].bitcast(I32),
                in_=w_scales[:, 4 * quadrant : 4 * quadrant + 4, :].rearrange("v r n -> r v n").bitcast(I32),
            )
        load_x(3)
        load(out=gain_q[:], in_=gain.rearrange("(v p j) -> p v j", p=P, j=J))
        load(out=hid[0][:], in_=hid_rows[0])
        load_w(1)
        load(out=b_wrd[:].bitcast(I32), in_=beta_words[0].bitcast(I32))
        for quadrant in range(4):
            load(
                out=b_scl[32 * quadrant : 32 * quadrant + 4, :].bitcast(I32),
                in_=beta_scales[0][4 * quadrant : 4 * quadrant + 4, :].bitcast(I32),
            )
        load(out=hid[1][:], in_=hid_rows[1])
        load(out=tgt[0][:], in_=tgt_rows[0])
        load(out=tgt[1][:], in_=tgt_rows[1])
        load(out=tau_b[:], in_=tau.partition_broadcast(P))

        with tc.manual_schedule():
            for r in range(-3, ROW_TILES + 2):
                if r + 3 == 0:
                    x_widen(nc.vector.tensor_copy, 0, 0, 512)
                    x_widen(nc.scalar.copy, 0, 512, D)
                elif r + 3 == 1:
                    x_widen(nc.vector.tensor_copy, 1, 0, D)
                elif r + 3 < ROW_TILES:
                    x_widen(nc.scalar.copy, r + 3, 0, D)
                if 0 <= r + 1 < ROW_TILES:
                    x_turn(r + 1)
                if 0 <= r - 5 < 4:
                    g_turn(r - 5)
                    g_copy_out(r - 5)
                if 0 <= r < ROW_TILES:
                    x_scale_out(r, 0)
                if 0 <= r - 1 < SINGLE_ROW_TILES:
                    x_quantise(r - 1)
                elif SINGLE_ROW_TILES < r <= ROW_TILES and r % 2 == 0:
                    x_quantise_pair(r // 2 - 1)
                if 0 <= r < ROW_TILES:
                    x_scale_out(r, 1)
                if 0 <= r - 2:
                    preact(r - 2, 0)
                    tanh(r - 2, 0)
                if 0 <= r - 5 < 2:
                    preact(r - 5, 1)
                    tanh(r - 5, 1)
                if r == 7:
                    apply_gain(0, 0, 0)
                if r == 8:
                    g_quantise(0)

            beta_product(0, 0)
            beta_product(0, 1)
            for step in range(0, 8, 2):
                pair = (divmod(step, 4), divmod(step + 1, 4))
                ahead = (step + 2, step + 3) if step < 6 else ()
                for k in ahead:
                    preact(k, 1)
                for k in ahead:
                    beta_product(*divmod(k, 4))
                for k in ahead:
                    tanh(k, 1)
                for v, nb in pair:
                    h_turn(0, v, nb)
                if step < 6:
                    apply_gain(0, *divmod(step // 2 + 1, 2))
                if step == 0:
                    g_quantise(1)
                for v, qb in pair:
                    residual(v, qb)
                for v, nb in pair:
                    energy(0, v, nb)
                if step == 4:
                    e_quantise(0)
                else:
                    if step > 0:
                        hs_quantise(0, step // 4, 0, NODE_HALF)
            e_quantise(1)

            for step in range(0, 8, 2):
                pair = (divmod(step, 4), divmod(step + 1, 4))
                for v, nb in pair:
                    h_turn(1, v, nb)
                blocks = (step - 2, step - 1) if step in (2, 4) else ()
                for nb in blocks:
                    correlate(0, nb)
                for v, nb in pair:
                    energy(1, v, nb)
                for nb in blocks:
                    square(0, nb)
            apply_gain(1, 0, 0)
            apply_gain(1, 0, 1)
            energy_inverse(0)
            apply_gain(1, 1, 0)
            hs_quantise(1, 0, 0, NODE_HALF)
            apply_gain(1, 1, 1)
            hs_quantise(1, 1, 0, 256)
            hs_quantise(1, 1, 256, NODE_HALF)

            for nb in (0, 1):
                correlate(1, nb)
                square(1, nb)
            for nb in (0, 1, 2):
                score(0, nb)
            energy_inverse(1)
            score(0, 3)
            for nb in range(4):
                if nb + 2 < 4:
                    correlate(1, nb + 2)
                    square(1, nb + 2)
                score(1, nb, parts=LAST_BLOCK_PARTS if nb == 3 else 1)
